import numpy as np
import ml_dtypes


def mxq(x, axis, fmt="e4m3"):
    dtype, down = {"e4m3": (ml_dtypes.float8_e4m3fn, 7), "e5m2": (ml_dtypes.float8_e5m2, 14)}[fmt]
    v = np.moveaxis(np.asarray(x, np.float32).astype(ml_dtypes.bfloat16).astype(np.float64), axis, -1)
    blocks = v.reshape(v.shape[:-1] + (-1, 32))
    amax = np.abs(blocks).max(-1, keepdims=True)
    byte = np.maximum(np.where(amax > 0, np.frexp(amax)[1] - 1 + 127, 0) - down, 1)
    scale = np.exp2(byte - 127.0)
    codes = (blocks / scale).astype(np.float32).astype(dtype).astype(np.float64)
    return np.moveaxis((codes * scale).reshape(v.shape), -1, axis)


WIDE = False


def mx_kscale(k):
    if not WIDE:
        return np.ones(k)
    levels = np.array([24, -24, 12, -12, 0])
    if k % 512:
        return np.exp2(np.random.permutation(np.resize(levels, k // 32))).repeat(32)
    a = np.empty((k // 512, 16))
    for p in range(k // 512):
        a[p, :8] = np.random.permutation(np.resize(levels, 8))
        for g in range(8):
            far = levels[np.abs(levels - a[p, g]) >= 10]
            a[p, g + 8] = far[np.random.randint(len(far))]
    return np.exp2(a.ravel()).repeat(32)


def f64(x):
    return np.asarray(x).astype(np.float64)


def striped(idx):
    return np.tile(idx.reshape(-1, 16).T, (8, 1)).astype(np.uint16)


def unstriped(offs):
    return offs[:16].T.reshape(-1).astype(np.int64)


E2M1 = np.array([0.0, 0.5, 1.0, 1.5, 2.0, 3.0, 4.0, 6.0, -0.0, -0.5, -1.0, -1.5, -2.0, -3.0, -4.0, -6.0])


def pack_weight(w, fmt):
    k, n = w.shape
    w = f64(np.asarray(w, np.float32).astype(ml_dtypes.bfloat16)).reshape(k // 32, 32, n)
    amax = np.abs(w).max(1)
    if fmt == "e4m3":
        byte = np.frexp(amax)[1] - 1 + 127 - 7
    else:
        mant, ex = np.frexp(amax / 6.0)
        byte = np.where(mant > 0.5, ex, ex - 1) + 127
    byte = np.clip(np.where(amax > 0, byte, 1), 1, 254)
    scaled = (w * np.exp2(127.0 - byte)[:, None, :]).reshape(k, n).astype(np.float32)
    by_word = np.ascontiguousarray(scaled.reshape(k // 512, 128, 4, n).transpose(0, 1, 3, 2))
    if fmt == "e4m3":
        words = by_word.astype(ml_dtypes.float8_e4m3fn).view(np.uint8)
    else:
        c = by_word.astype(ml_dtypes.float4_e2m1fn).view(np.uint8) & 0xF
        words = (c[..., 0::2] | (c[..., 1::2] << 4)).reshape(k // 512, 128, 2 * n)
    return np.ascontiguousarray(words), np.ascontiguousarray(byte.astype(np.uint8).reshape(k // 512, 16, n))


def unpack_weight(words, scales, fmt):
    g, _, n = scales.shape
    words = np.ascontiguousarray(words).reshape(g, 128, n, -1)
    if fmt == "e4m3":
        vals = words.view(ml_dtypes.float8_e4m3fn).astype(np.float64)
    else:
        nib = np.empty((g, 128, n, 4), np.uint8)
        nib[..., 0::2] = words & 0xF
        nib[..., 1::2] = words >> 4
        vals = E2M1[nib]
    vals = vals * np.repeat(np.exp2(scales.astype(np.float64) - 127.0), 8, axis=1)[..., None]
    return vals.transpose(0, 1, 3, 2).reshape(g * 512, n)


def pack_table4(v):
    words, scales = pack_weight(v, "e2m1")
    g, t = words.shape[0] // 2, v.shape[1]
    return np.ascontiguousarray(words.reshape(g, 2, 128, t, 2).transpose(0, 2, 3, 1, 4).reshape(g, 128, t, 4)), scales


def unpack_table4(words, scales):
    g, _, t, _ = words.shape
    return unpack_weight(words.reshape(g, 128, t, 2, 2).transpose(0, 3, 1, 2, 4).reshape(2 * g, 128, 2 * t), scales, "e2m1")


K, R, M, T, N, J = 1024, 1024, 256, 1024, 256, 512


def setup_inputs():
    n = np.random.standard_normal
    u = mx_kscale(R)[:, None]
    s = mx_kscale(K)[:, None]
    wv = n((R, N)) / np.sqrt(R) / u
    p_w4 = pack_weight(n((K, R)) / np.sqrt(K) / s / u.T, "e2m1")
    p_tab = pack_table4(n((R, T)) * u)
    p_wv4 = pack_weight(wv[512:], "e2m1")
    return {
        "x": (n((K, M)) * s).astype(np.float32),
        "w4_words": p_w4[0],
        "w4_scales": p_w4[1],
        "tab_words": p_tab[0],
        "tab_scales": p_tab[1],
        "wv8": (wv[:512]).astype(np.float32),
        "wv4_words": p_wv4[0],
        "wv4_scales": p_wv4[1],
        "msk": (np.where(np.random.rand(M, J) < 0.2, -4.0, 0.0)).astype(np.float32),
        "offs": striped(np.random.permutation(T)[:J]),
    }


def reference(x, w4_words, w4_scales, tab_words, tab_scales, wv8, wv4_words, wv4_scales, msk, offs):
    idx = unstriped(offs)
    x_ = mxq(f64(x), 0, "e4m3")
    w4_ = unpack_weight(w4_words, w4_scales, "e2m1")
    qa = w4_.T @ x_
    qa_ = mxq(qa, 0, "e4m3")
    tab_ = unpack_table4(tab_words, tab_scales)[:, idx]
    sc = qa_.T @ tab_
    wv8_ = mxq(f64(wv8), 0, "e4m3")
    wv4_ = unpack_weight(wv4_words, wv4_scales, "e2m1")
    vv = wv8_.T @ tab_[:512] + wv4_.T @ tab_[512:]
    return sc * 0.03125 + f64(msk), vv

@@ -1,0 +1,187 @@
+from contextlib import ExitStack
+
+import concourse.mybir as mybir
+from concourse.masks import make_identity
+
+K, R, M, T, N, J = 1024, 1024, 256, 1024, 256, 512
+FLOPS = 2 * K * R * M + 2 * R * M * J + 2 * R * N * J
+
+F32 = mybir.dt.float32
+BF16 = mybir.dt.bfloat16
+I32 = mybir.dt.int32
+U32 = mybir.dt.uint32
+U16 = mybir.dt.uint16
+U8 = mybir.dt.uint8
+FP8X4 = mybir.dt.float8_e4m3fn_x4
+FP4X4 = mybir.dt.float4_e2m1fn_x4
+MULT = mybir.AluOpType.mult
+ADD = mybir.AluOpType.add
+
+P = 128
+PACK = 4
+KP = P * PACK
+SCORE_SCALE = 0.03125
+
+
+def load_scale_rows(queue, planes, scales):
+    rows = scales.bitcast(I32).rearrange("a (q r) n -> r q a n", r=4)
+    for r in range(4):
+        queue.dma_start(out=planes[r:P:32, :, :].bitcast(I32), in_=rows[r])
+
+
+def round_and_interleave(copy, grouped, raw):
+    copy(
+        out=grouped.rearrange("p (c i) t -> p c t i", i=4),
+        in_=raw.rearrange("p t (c i) -> p c t i", i=4),
+    )
+
+
+def tile_list_mlat_qf_mask_kernel(
+    tc, x, w4_words, w4_scales, tab_words, tab_scales, wv8, wv4_words, wv4_scales, msk, offs, out_0, out_1
+):
+    nc = tc.nc
+    with ExitStack() as ctx:
+        sb = ctx.enter_context(tc.tile_pool(name="sb", bufs=1))
+        ps = ctx.enter_context(tc.psum_pool(name="ps", bufs=1))
+
+        offsets = sb.tile([P, J // 16], U16, name="offsets")
+        tab_s = sb.tile([P, 2, T], U8, name="tab_s", align_bytes=64)
+        w4_s = sb.tile([P, 2, R], U8, name="w4_s", align_bytes=64)
+        wv4_s = sb.tile([P, 1, N], U8, name="wv4_s", align_bytes=64)
+        x_raw = [sb.tile([P, PACK, M], F32, name=f"x_raw{a}") for a in range(2)]
+        w4_w = [sb.tile([P, 2 * R], U8, name=f"w4_w{a}", align_bytes=64) for a in range(2)]
+        tab_w = sb.tile([P, T], I32, name="tab_w", align_bytes=64)
+        wv8_raw = sb.tile([P, PACK, N], F32, name="wv8_raw")
+        wv4_w = sb.tile([P, 2 * N], U8, name="wv4_w", align_bytes=64)
+        mask = sb.tile([P, 2, J], F32, name="mask")
+        ident = sb.tile([P, P], F32, name="ident")
+
+        nc.vector.memset(tab_s[:].bitcast(I32), 0)
+        nc.vector.memset(w4_s[:].bitcast(I32), 0)
+        nc.gpsimd.memset(wv4_s[:].bitcast(I32), 0)
+
+        def x_rows(a):
+            return x[a * KP : (a + 1) * KP, :].rearrange("(p t) m -> p t m", t=PACK)
+
+        nc.sync.dma_start(offsets[:], offs)
+        nc.sync.dma_start(out=x_raw[0][:], in_=x_rows(0))
+        load_scale_rows(nc.sync, tab_s, tab_scales)
+        load_scale_rows(nc.sync, w4_s, w4_scales)
+        load_scale_rows(nc.gpsimd, wv4_s, wv4_scales)
+        make_identity(nc, ident[:])
+        nc.sync.dma_start(out=w4_w[0][:].bitcast(I32), in_=w4_words[0].bitcast(I32))
+        nc.sync.dma_start(out=x_raw[1][:], in_=x_rows(1))
+        nc.sync.dma_start(out=tab_w[:], in_=tab_words[0].rearrange("p t b -> p (t b)").bitcast(I32))
+        nc.sync.dma_start(out=w4_w[1][:].bitcast(I32), in_=w4_words[1].bitcast(I32))
+        nc.sync.dma_start(out=wv8_raw[:], in_=wv8.rearrange("(p t) n -> p t n", t=PACK))
+        nc.sync.dma_start(out=wv4_w[:].bitcast(I32), in_=wv4_words[0].bitcast(I32))
+        nc.sync.dma_start(out=mask[:], in_=msk.rearrange("(h p) j -> p h j", p=P))
+
+        def quantize(name, grouped, width):
+            codes = sb.tile([P, width], U32, name=name + "_c", align_bytes=64)
+            scales = sb.tile([P, width], U8, name=name + "_s", align_bytes=64)
+            nc.vector.quantize_mx(out=codes[:].bitcast(FP8X4), scales=scales[:], in_=grouped)
+            return codes, scales
+
+        x_q = {}
+        qa_t = {}
+
+        def quantize_x(a, engines):
+            grouped = []
+            for h in range(2):
+                g = sb.tile([P, P, PACK], BF16, name=f"x_g{a}{h}", align_bytes=64)
+                round_and_interleave(engines[h], g[:], x_raw[a][:, :, h * P : (h + 1) * P])
+                grouped.append(g)
+            for h in (1, 0) if a == 0 else (0, 1):
+                x_q[a, h] = quantize(f"x{a}{h}", grouped[h][:].rearrange("p m t -> p (m t)"), P)
+
+        def project(a):
+            for h in range(2):
+                for b in range(2):
+                    if a == 0:
+                        qa_t[h, b] = ps.tile([P, KP], F32, name=f"qa_t{h}{b}", tag=f"bank{2 * h + b}")
+                    codes, scales = x_q[a, h]
+                    nc.tensor.matmul_mx(
+                        out=qa_t[h, b][:],
+                        lhsT=codes[:].bitcast(FP8X4),
+                        lhsT_scale=scales[:],
+                        rhs=w4_w[a][:, 2 * KP * b : 2 * KP * (b + 1)].bitcast(FP4X4),
+                        rhs_scale=w4_s[:, a, KP * b : KP * (b + 1)],
+                        start=(a == 0),
+                        stop=(a == 1),
+                    )
+
+        picked_s = sb.tile([P, 2, J], U8, name="picked_s", align_bytes=64)
+        picked_pairs = sb.tile([P, J], U32, name="picked_pairs", align_bytes=64)
+        picked_w = sb.tile([P, 2, J], U16, name="picked_w", align_bytes=64)
+
+        quantize_x(0, (nc.scalar.copy, nc.vector.tensor_copy))
+        project(0)
+        quantize_x(1, (nc.scalar.copy, nc.scalar.copy))
+        project(1)
+        for b in range(2):
+            nc.vector.tensor_copy(picked_s[:, b, :], tab_s[:, b, :].indirect(offsets[:]))
+        nc.vector.tensor_copy(picked_pairs[:], tab_w[:].bitcast(U32).indirect(offsets[:]))
+        nc.vector.tensor_copy(out=picked_w[:], in_=picked_pairs[:].bitcast(U16).rearrange("p (j d) -> p d j", d=2))
+
+        qa_q = {}
+        for h in range(2):
+            rounded = {}
+            for b in range(2):
+                rounded[b] = sb.tile([P, 2, P, 2], BF16, name=f"qa_r{h}{b}", align_bytes=64)
+                copy = nc.scalar.copy if b == 0 else nc.vector.tensor_copy
+                copy(out=rounded[b][:], in_=qa_t[h, b][:].rearrange("m (p u e) -> m u p e", u=2, e=2))
+            for b in range(2):
+                pairs = rounded[b][:].rearrange("m u p e -> m (u p e)").bitcast(F32)
+                turned = ps.tile([P, 2, P], F32, name=f"turned{h}{b}", tag=f"turn{b}")
+                for u in range(2):
+                    nc.tensor.transpose(turned[:, u, :], pairs[:, u * P : (u + 1) * P], ident[:])
+                grouped = sb.tile([P, P, PACK], BF16, name=f"qa_g{h}{b}", align_bytes=64)
+                nc.scalar.copy(out=grouped[:].bitcast(F32), in_=turned[:].rearrange("p u m -> p m u"))
+                qa_q[h, b] = quantize(f"qa{h}{b}", grouped[:].rearrange("p m t -> p (m t)"), P)
+
+        for h in range(2):
+            sc = ps.tile([P, J], F32, name=f"sc{h}", tag=f"bank{h}")
+            for b in range(2):
+                codes, scales = qa_q[h, b]
+                nc.tensor.matmul_mx(
+                    out=sc[:],
+                    lhsT=codes[:].bitcast(FP8X4),
+                    lhsT_scale=scales[:],
+                    rhs=picked_w[:, b, :].bitcast(FP4X4),
+                    rhs_scale=picked_s[:, b, :],
+                    start=(b == 0),
+                    stop=(b == 1),
+                )
+            scores = sb.tile([P, J], F32, name=f"scores{h}")
+            nc.vector.scalar_tensor_tensor(
+                out=scores[:], in0=sc[:], scalar=SCORE_SCALE, in1=mask[:, h, :], op0=MULT, op1=ADD
+            )
+            nc.sync.dma_start(out=out_0[h * P : (h + 1) * P, :], in_=scores[:])
+
+        wv8_g = sb.tile([P, N, PACK], BF16, name="wv8_g", align_bytes=64)
+        round_and_interleave(nc.scalar.copy, wv8_g[:], wv8_raw[:])
+        wv8_c, wv8_s = quantize("wv8", wv8_g[:].rearrange("p n t -> p (n t)"), N)
+        for g in range(2):
+            vv = ps.tile([P, J], F32, name=f"vv{g}", tag=f"value{g}")
+            nc.tensor.matmul_mx(
+                out=vv[:],
+                lhsT=wv4_w[:, 2 * P * g : 2 * P * (g + 1)].bitcast(FP4X4),
+                lhsT_scale=wv4_s[:, 0, P * g : P * (g + 1)],
+                rhs=picked_w[:, 1, :].bitcast(FP4X4),
+                rhs_scale=picked_s[:, 1, :],
+                start=True,
+                stop=False,
+            )
+            nc.tensor.matmul_mx(
+                out=vv[:],
+                lhsT=wv8_c[:, P * g : P * (g + 1)].bitcast(FP8X4),
+                lhsT_scale=wv8_s[:, P * g : P * (g + 1)],
+                rhs=picked_w[:, 0, :].bitcast(FP4X4),
+                rhs_scale=picked_s[:, 0, :],
+                start=False,
+                stop=True,
+            )
+            values = sb.tile([P, J], F32, name=f"values{g}")
+            nc.scalar.copy(out=values[:], in_=vv[:])
+            nc.sync.dma_start(out=out_1[g * P : (g + 1) * P, :], in_=values[:])

@@ -49,7 +49,7 @@ def tile_list_mlat_qf_mask_kernel(
         w4_s = sb.tile([P, 2, R], U8, name="w4_s", align_bytes=64)
         wv4_s = sb.tile([P, 1, N], U8, name="wv4_s", align_bytes=64)
         x_raw = [sb.tile([P, PACK, M], F32, name=f"x_raw{a}") for a in range(2)]
-        w4_w = [sb.tile([P, 2 * R], U8, name=f"w4_w{a}", align_bytes=64) for a in range(2)]
+        w4_w = [sb.tile([P, 2, 2 * KP], U8, name=f"w4_w{b}", align_bytes=64) for b in range(2)]
         tab_w = sb.tile([P, T], I32, name="tab_w", align_bytes=64)
         wv8_raw = sb.tile([P, PACK, N], F32, name="wv8_raw")
         wv4_w = sb.tile([P, 2 * N], U8, name="wv4_w", align_bytes=64)
@@ -58,24 +58,37 @@ def tile_list_mlat_qf_mask_kernel(
 
         nc.vector.memset(tab_s[:].bitcast(I32), 0)
         nc.vector.memset(w4_s[:].bitcast(I32), 0)
+        make_identity(nc, ident[:])
         nc.gpsimd.memset(wv4_s[:].bitcast(I32), 0)
 
-        def x_rows(a):
-            return x[a * KP : (a + 1) * KP, :].rearrange("(p t) m -> p t m", t=PACK)
+        def load_x(a):
+            rows = x[a * KP : (a + 1) * KP, :].rearrange("(p t) m -> p t m", t=PACK)
+            nc.sync.dma_start(out=x_raw[a][:], in_=rows)
+
+        def load_w4(b):
+            words = w4_words.rearrange("a p c -> p a c")[:, :, 2 * KP * b : 2 * KP * (b + 1)]
+            nc.sync.dma_start(out=w4_w[b][:].bitcast(I32), in_=words.bitcast(I32))
 
         nc.sync.dma_start(offsets[:], offs)
-        nc.sync.dma_start(out=x_raw[0][:], in_=x_rows(0))
+        load_w4(0)
         load_scale_rows(nc.sync, tab_s, tab_scales)
+        load_x(0)
+        load_x(1)
         load_scale_rows(nc.sync, w4_s, w4_scales)
-        load_scale_rows(nc.gpsimd, wv4_s, wv4_scales)
-        make_identity(nc, ident[:])
-        nc.sync.dma_start(out=w4_w[0][:].bitcast(I32), in_=w4_words[0].bitcast(I32))
-        nc.sync.dma_start(out=x_raw[1][:], in_=x_rows(1))
         nc.sync.dma_start(out=tab_w[:], in_=tab_words[0].rearrange("p t b -> p (t b)").bitcast(I32))
-        nc.sync.dma_start(out=w4_w[1][:].bitcast(I32), in_=w4_words[1].bitcast(I32))
+        load_w4(1)
         nc.sync.dma_start(out=wv8_raw[:], in_=wv8.rearrange("(p t) n -> p t n", t=PACK))
         nc.sync.dma_start(out=wv4_w[:].bitcast(I32), in_=wv4_words[0].bitcast(I32))
+        load_scale_rows(nc.sync, wv4_s, wv4_scales)
         nc.sync.dma_start(out=mask[:], in_=msk.rearrange("(h p) j -> p h j", p=P))
+
+        primer = sb.tile([P, 8], F32, name="primer")
+        nc.scalar.copy(out=primer[:], in_=ident[:, 0:8])
+        warm = ps.tile([P, 4, P], F32, name="warm", tag="turn11")
+        for i in range(24):
+            nc.tensor.transpose(warm[:, i % 4, :], ident[:], ident[:])
+        for i in range(8):
+            nc.tensor.transpose(warm[:, i % 4, :], x_raw[0][:, i % 4, 0:P], ident[:])
 
         def quantize(name, grouped, width):
             codes = sb.tile([P, width], U32, name=name + "_c", align_bytes=64)
@@ -83,89 +96,79 @@ def tile_list_mlat_qf_mask_kernel(
             nc.vector.quantize_mx(out=codes[:].bitcast(FP8X4), scales=scales[:], in_=grouped)
             return codes, scales
 
-        x_q = {}
-        qa_t = {}
-
-        def quantize_x(a, engines):
-            grouped = []
-            for h in range(2):
-                g = sb.tile([P, P, PACK], BF16, name=f"x_g{a}{h}", align_bytes=64)
-                round_and_interleave(engines[h], g[:], x_raw[a][:, :, h * P : (h + 1) * P])
-                grouped.append(g)
-            for h in (1, 0) if a == 0 else (0, 1):
-                x_q[a, h] = quantize(f"x{a}{h}", grouped[h][:].rearrange("p m t -> p (m t)"), P)
-
-        def project(a):
-            for h in range(2):
-                for b in range(2):
-                    if a == 0:
-                        qa_t[h, b] = ps.tile([P, KP], F32, name=f"qa_t{h}{b}", tag=f"bank{2 * h + b}")
-                    codes, scales = x_q[a, h]
-                    nc.tensor.matmul_mx(
-                        out=qa_t[h, b][:],
-                        lhsT=codes[:].bitcast(FP8X4),
-                        lhsT_scale=scales[:],
-                        rhs=w4_w[a][:, 2 * KP * b : 2 * KP * (b + 1)].bitcast(FP4X4),
-                        rhs_scale=w4_s[:, a, KP * b : KP * (b + 1)],
-                        start=(a == 0),
-                        stop=(a == 1),
-                    )
-
         picked_s = sb.tile([P, 2, J], U8, name="picked_s", align_bytes=64)
         picked_pairs = sb.tile([P, J], U32, name="picked_pairs", align_bytes=64)
         picked_w = sb.tile([P, 2, J], U16, name="picked_w", align_bytes=64)
 
-        quantize_x(0, (nc.scalar.copy, nc.vector.tensor_copy))
-        project(0)
-        quantize_x(1, (nc.scalar.copy, nc.scalar.copy))
-        project(1)
+        x_q = {}
+        for a in range(2):
+            for h in range(2):
+                copy = nc.vector.tensor_copy if (a, h) == (1, 0) else nc.scalar.copy
+                grouped = sb.tile([P, P, PACK], BF16, name=f"x_g{a}{h}", align_bytes=64)
+                round_and_interleave(copy, grouped[:], x_raw[a][:, :, h * P : (h + 1) * P])
+                x_q[a, h] = quantize(f"x{a}{h}", grouped[:].rearrange("p m t -> p (m t)"), P)
+
         for b in range(2):
             nc.vector.tensor_copy(picked_s[:, b, :], tab_s[:, b, :].indirect(offsets[:]))
+
+        units = [(h, b) for b in range(2) for h in range(2)]
+        qa_t = {}
+        for h, b in units:
+            qa_t[h, b] = ps.tile([P, KP], F32, name=f"qa_t{h}{b}", tag=f"bank{h}{b}")
+            for a in range(2):
+                codes, scales = x_q[a, h]
+                nc.tensor.matmul_mx(
+                    out=qa_t[h, b][:],
+                    lhsT=codes[:].bitcast(FP8X4),
+                    lhsT_scale=scales[:],
+                    rhs=w4_w[b][:, a, :].bitcast(FP4X4),
+                    rhs_scale=w4_s[:, a, KP * b : KP * (b + 1)],
+                    start=(a == 0),
+                    stop=(a == 1),
+                )
+
+        rounded = {}
+        for h, b in units:
+            rounded[h, b] = sb.tile([P, 2, P, 2], BF16, name=f"qa_r{h}{b}", align_bytes=64)
+            nc.scalar.copy(out=rounded[h, b][:], in_=qa_t[h, b][:].rearrange("m (p u e) -> m u p e", u=2, e=2))
+        qa_g = {}
+        for h, b in units:
+            pairs = rounded[h, b][:].rearrange("m u p e -> m (u p e)").bitcast(F32)
+            turned = ps.tile([P, 2, P], F32, name=f"turned{h}{b}", tag=f"turn{h}{b}")
+            for u in range(2):
+                nc.tensor.transpose(turned[:, u, :], pairs[:, u * P : (u + 1) * P], ident[:])
+            qa_g[h, b] = sb.tile([P, P, PACK], BF16, name=f"qa_g{h}{b}", align_bytes=64)
+            nc.scalar.copy(out=qa_g[h, b][:].bitcast(F32), in_=turned[:].rearrange("p u m -> p m u"))
+
         nc.vector.tensor_copy(picked_pairs[:], tab_w[:].bitcast(U32).indirect(offsets[:]))
         nc.vector.tensor_copy(out=picked_w[:], in_=picked_pairs[:].bitcast(U16).rearrange("p (j d) -> p d j", d=2))
 
-        qa_q = {}
+        sc = [ps.tile([P, J], F32, name=f"sc{h}", tag=f"bank{h}0") for h in range(2)]
+        for h, b in units:
+            codes, scales = quantize(f"qa{h}{b}", qa_g[h, b][:].rearrange("p m t -> p (m t)"), P)
+            nc.tensor.matmul_mx(
+                out=sc[h][:],
+                lhsT=codes[:].bitcast(FP8X4),
+                lhsT_scale=scales[:],
+                rhs=picked_w[:, b, :].bitcast(FP4X4),
+                rhs_scale=picked_s[:, b, :],
+                start=(b == 0),
+                stop=(b == 1),
+            )
         for h in range(2):
-            rounded = {}
-            for b in range(2):
-                rounded[b] = sb.tile([P, 2, P, 2], BF16, name=f"qa_r{h}{b}", align_bytes=64)
-                copy = nc.scalar.copy if b == 0 else nc.vector.tensor_copy
-                copy(out=rounded[b][:], in_=qa_t[h, b][:].rearrange("m (p u e) -> m u p e", u=2, e=2))
-            for b in range(2):
-                pairs = rounded[b][:].rearrange("m u p e -> m (u p e)").bitcast(F32)
-                turned = ps.tile([P, 2, P], F32, name=f"turned{h}{b}", tag=f"turn{b}")
-                for u in range(2):
-                    nc.tensor.transpose(turned[:, u, :], pairs[:, u * P : (u + 1) * P], ident[:])
-                grouped = sb.tile([P, P, PACK], BF16, name=f"qa_g{h}{b}", align_bytes=64)
-                nc.scalar.copy(out=grouped[:].bitcast(F32), in_=turned[:].rearrange("p u m -> p m u"))
-                qa_q[h, b] = quantize(f"qa{h}{b}", grouped[:].rearrange("p m t -> p (m t)"), P)
-
-        for h in range(2):
-            sc = ps.tile([P, J], F32, name=f"sc{h}", tag=f"bank{h}")
-            for b in range(2):
-                codes, scales = qa_q[h, b]
-                nc.tensor.matmul_mx(
-                    out=sc[:],
-                    lhsT=codes[:].bitcast(FP8X4),
-                    lhsT_scale=scales[:],
-                    rhs=picked_w[:, b, :].bitcast(FP4X4),
-                    rhs_scale=picked_s[:, b, :],
-                    start=(b == 0),
-                    stop=(b == 1),
-                )
             scores = sb.tile([P, J], F32, name=f"scores{h}")
             nc.vector.scalar_tensor_tensor(
-                out=scores[:], in0=sc[:], scalar=SCORE_SCALE, in1=mask[:, h, :], op0=MULT, op1=ADD
+                out=scores[:], in0=sc[h][:], scalar=SCORE_SCALE, in1=mask[:, h, :], op0=MULT, op1=ADD
             )
             nc.sync.dma_start(out=out_0[h * P : (h + 1) * P, :], in_=scores[:])
 
         wv8_g = sb.tile([P, N, PACK], BF16, name="wv8_g", align_bytes=64)
-        round_and_interleave(nc.scalar.copy, wv8_g[:], wv8_raw[:])
+        round_and_interleave(nc.vector.tensor_copy, wv8_g[:], wv8_raw[:])
         wv8_c, wv8_s = quantize("wv8", wv8_g[:].rearrange("p n t -> p (n t)"), N)
+        vv = [ps.tile([P, J], F32, name=f"vv{g}", tag=f"turn{g}0") for g in range(2)]
         for g in range(2):
-            vv = ps.tile([P, J], F32, name=f"vv{g}", tag=f"value{g}")
             nc.tensor.matmul_mx(
-                out=vv[:],
+                out=vv[g][:],
                 lhsT=wv4_w[:, 2 * P * g : 2 * P * (g + 1)].bitcast(FP4X4),
                 lhsT_scale=wv4_s[:, 0, P * g : P * (g + 1)],
                 rhs=picked_w[:, 1, :].bitcast(FP4X4),
@@ -174,7 +177,7 @@ def tile_list_mlat_qf_mask_kernel(
                 stop=False,
             )
             nc.tensor.matmul_mx(
-                out=vv[:],
+                out=vv[g][:],
                 lhsT=wv8_c[:, P * g : P * (g + 1)].bitcast(FP8X4),
                 lhsT_scale=wv8_s[:, P * g : P * (g + 1)],
                 rhs=picked_w[:, 0, :].bitcast(FP4X4),
@@ -183,5 +186,5 @@ def tile_list_mlat_qf_mask_kernel(
                 stop=True,
             )
             values = sb.tile([P, J], F32, name=f"values{g}")
-            nc.scalar.copy(out=values[:], in_=vv[:])
+            nc.scalar.copy(out=values[:], in_=vv[g][:])
             nc.sync.dma_start(out=out_1[g * P : (g + 1) * P, :], in_=values[:])

@@ -50,7 +50,7 @@ def tile_list_mlat_qf_mask_kernel(
         wv4_s = sb.tile([P, 1, N], U8, name="wv4_s", align_bytes=64)
         x_raw = [sb.tile([P, PACK, M], F32, name=f"x_raw{a}") for a in range(2)]
         w4_w = [sb.tile([P, 2, 2 * KP], U8, name=f"w4_w{b}", align_bytes=64) for b in range(2)]
-        tab_w = sb.tile([P, T], I32, name="tab_w", align_bytes=64)
+        tab_w = sb.tile([P, T], I32, name="tab_w", tag="tab_w", align_bytes=64)
         wv8_raw = sb.tile([P, PACK, N], F32, name="wv8_raw")
         wv4_w = sb.tile([P, 2 * N], U8, name="wv4_w", align_bytes=64)
         mask = sb.tile([P, 2, J], F32, name="mask")
@@ -82,10 +82,10 @@ def tile_list_mlat_qf_mask_kernel(
         load_scale_rows(nc.sync, wv4_s, wv4_scales)
         nc.sync.dma_start(out=mask[:], in_=msk.rearrange("(h p) j -> p h j", p=P))
 
-        primer = sb.tile([P, 8], F32, name="primer")
+        primer = sb.tile([P, 8], BF16, name="primer")
         nc.scalar.copy(out=primer[:], in_=ident[:, 0:8])
         warm = ps.tile([P, 4, P], F32, name="warm", tag="turn11")
-        for i in range(24):
+        for i in range(22):
             nc.tensor.transpose(warm[:, i % 4, :], ident[:], ident[:])
         for i in range(8):
             nc.tensor.transpose(warm[:, i % 4, :], x_raw[0][:, i % 4, 0:P], ident[:])
@@ -97,14 +97,13 @@ def tile_list_mlat_qf_mask_kernel(
             return codes, scales
 
         picked_s = sb.tile([P, 2, J], U8, name="picked_s", align_bytes=64)
-        picked_pairs = sb.tile([P, J], U32, name="picked_pairs", align_bytes=64)
         picked_w = sb.tile([P, 2, J], U16, name="picked_w", align_bytes=64)
 
         x_q = {}
         for a in range(2):
             for h in range(2):
                 copy = nc.vector.tensor_copy if (a, h) == (1, 0) else nc.scalar.copy
-                grouped = sb.tile([P, P, PACK], BF16, name=f"x_g{a}{h}", align_bytes=64)
+                grouped = sb.tile([P, P, PACK], BF16, name=f"x_g{a}{h}", tag=f"x_g{a * h}{h}", align_bytes=64)
                 round_and_interleave(copy, grouped[:], x_raw[a][:, :, h * P : (h + 1) * P])
                 x_q[a, h] = quantize(f"x{a}{h}", grouped[:].rearrange("p m t -> p (m t)"), P)
 
@@ -115,17 +114,18 @@ def tile_list_mlat_qf_mask_kernel(
         qa_t = {}
         for h, b in units:
             qa_t[h, b] = ps.tile([P, KP], F32, name=f"qa_t{h}{b}", tag=f"bank{h}{b}")
-            for a in range(2):
-                codes, scales = x_q[a, h]
-                nc.tensor.matmul_mx(
-                    out=qa_t[h, b][:],
-                    lhsT=codes[:].bitcast(FP8X4),
-                    lhsT_scale=scales[:],
-                    rhs=w4_w[b][:, a, :].bitcast(FP4X4),
-                    rhs_scale=w4_s[:, a, KP * b : KP * (b + 1)],
-                    start=(a == 0),
-                    stop=(a == 1),
-                )
+        passes = [(h, 0, a) for a in range(2) for h in range(2)] + [(h, 1, a) for h in range(2) for a in range(2)]
+        for h, b, a in passes:
+            codes, scales = x_q[a, h]
+            nc.tensor.matmul_mx(
+                out=qa_t[h, b][:],
+                lhsT=codes[:].bitcast(FP8X4),
+                lhsT_scale=scales[:],
+                rhs=w4_w[b][:, a, :].bitcast(FP4X4),
+                rhs_scale=w4_s[:, a, KP * b : KP * (b + 1)],
+                start=(a == 0),
+                stop=(a == 1),
+            )
 
         rounded = {}
         for h, b in units:
@@ -140,11 +140,39 @@ def tile_list_mlat_qf_mask_kernel(
             qa_g[h, b] = sb.tile([P, P, PACK], BF16, name=f"qa_g{h}{b}", align_bytes=64)
             nc.scalar.copy(out=qa_g[h, b][:].bitcast(F32), in_=turned[:].rearrange("p u m -> p m u"))
 
+        picked_pairs = sb.tile([P, J], U32, name="picked_pairs", tag="x_g11", align_bytes=64)
         nc.vector.tensor_copy(picked_pairs[:], tab_w[:].bitcast(U32).indirect(offsets[:]))
         nc.vector.tensor_copy(out=picked_w[:], in_=picked_pairs[:].bitcast(U16).rearrange("p (j d) -> p d j", d=2))
 
+        wv8_g = sb.tile([P, N, PACK], BF16, name="wv8_g", tag="tab_w", align_bytes=64)
+        round_and_interleave(nc.vector.tensor_copy, wv8_g[:], wv8_raw[:])
+        wv8_c, wv8_s = quantize("wv8", wv8_g[:].rearrange("p n t -> p (n t)"), N)
+        for g in range(2):
+            vv = ps.tile([P, J], F32, name=f"vv{g}", tag=f"bank{g}1")
+            nc.tensor.matmul_mx(
+                out=vv[:],
+                lhsT=wv4_w[:, 2 * P * g : 2 * P * (g + 1)].bitcast(FP4X4),
+                lhsT_scale=wv4_s[:, 0, P * g : P * (g + 1)],
+                rhs=picked_w[:, 1, :].bitcast(FP4X4),
+                rhs_scale=picked_s[:, 1, :],
+                start=True,
+                stop=False,
+            )
+            nc.tensor.matmul_mx(
+                out=vv[:],
+                lhsT=wv8_c[:, P * g : P * (g + 1)].bitcast(FP8X4),
+                lhsT_scale=wv8_s[:, P * g : P * (g + 1)],
+                rhs=picked_w[:, 0, :].bitcast(FP4X4),
+                rhs_scale=picked_s[:, 0, :],
+                start=False,
+                stop=True,
+            )
+            values = sb.tile([P, J], F32, name=f"values{g}")
+            nc.scalar.copy(out=values[:], in_=vv[:])
+            nc.sync.dma_start(out=out_1[g * P : (g + 1) * P, :], in_=values[:])
+
         sc = [ps.tile([P, J], F32, name=f"sc{h}", tag=f"bank{h}0") for h in range(2)]
-        for h, b in units:
+        for h, b in sorted(units):
             codes, scales = quantize(f"qa{h}{b}", qa_g[h, b][:].rearrange("p m t -> p (m t)"), P)
             nc.tensor.matmul_mx(
                 out=sc[h][:],
@@ -161,30 +189,3 @@ def tile_list_mlat_qf_mask_kernel(
                 out=scores[:], in0=sc[h][:], scalar=SCORE_SCALE, in1=mask[:, h, :], op0=MULT, op1=ADD
             )
             nc.sync.dma_start(out=out_0[h * P : (h + 1) * P, :], in_=scores[:])
-
-        wv8_g = sb.tile([P, N, PACK], BF16, name="wv8_g", align_bytes=64)
-        round_and_interleave(nc.vector.tensor_copy, wv8_g[:], wv8_raw[:])
-        wv8_c, wv8_s = quantize("wv8", wv8_g[:].rearrange("p n t -> p (n t)"), N)
-        vv = [ps.tile([P, J], F32, name=f"vv{g}", tag=f"turn{g}0") for g in range(2)]
-        for g in range(2):
-            nc.tensor.matmul_mx(
-                out=vv[g][:],
-                lhsT=wv4_w[:, 2 * P * g : 2 * P * (g + 1)].bitcast(FP4X4),
-                lhsT_scale=wv4_s[:, 0, P * g : P * (g + 1)],
-                rhs=picked_w[:, 1, :].bitcast(FP4X4),
-                rhs_scale=picked_s[:, 1, :],
-                start=True,
-                stop=False,
-            )
-            nc.tensor.matmul_mx(
-                out=vv[g][:],
-                lhsT=wv8_c[:, P * g : P * (g + 1)].bitcast(FP8X4),
-                lhsT_scale=wv8_s[:, P * g : P * (g + 1)],
-                rhs=picked_w[:, 0, :].bitcast(FP4X4),
-                rhs_scale=picked_s[:, 0, :],
-                start=False,
-                stop=True,
-            )
-            values = sb.tile([P, J], F32, name=f"values{g}")
-            nc.scalar.copy(out=values[:], in_=vv[g][:])
-            nc.sync.dma_start(out=out_1[g * P : (g + 1) * P, :], in_=values[:])

@@ -184,8 +184,10 @@ def tile_list_mlat_qf_mask_kernel(
                 stop=(b == 1),
             )
         for h in range(2):
-            scores = sb.tile([P, J], F32, name=f"scores{h}")
-            nc.vector.scalar_tensor_tensor(
-                out=scores[:], in0=sc[h][:], scalar=SCORE_SCALE, in1=mask[:, h, :], op0=MULT, op1=ADD
-            )
-            nc.sync.dma_start(out=out_0[h * P : (h + 1) * P, :], in_=scores[:])
+            for c in range(2):
+                cols = slice(c * J // 2, (c + 1) * J // 2)
+                scores = sb.tile([P, J // 2], F32, name=f"scores{h}{c}")
+                nc.vector.scalar_tensor_tensor(
+                    out=scores[:], in0=sc[h][:, cols], scalar=SCORE_SCALE, in1=mask[:, h, cols], op0=MULT, op1=ADD
+                )
+                nc.sync.dma_start(out=out_0[h * P : (h + 1) * P, cols], in_=scores[:])

@@ -58,8 +58,8 @@ def tile_list_mlat_qf_mask_kernel(
 
         nc.vector.memset(tab_s[:].bitcast(I32), 0)
         nc.vector.memset(w4_s[:].bitcast(I32), 0)
+        nc.vector.memset(wv4_s[:].bitcast(I32), 0)
         make_identity(nc, ident[:])
-        nc.gpsimd.memset(wv4_s[:].bitcast(I32), 0)
 
         def load_x(a):
             rows = x[a * KP : (a + 1) * KP, :].rearrange("(p t) m -> p t m", t=PACK)
@@ -90,8 +90,8 @@ def tile_list_mlat_qf_mask_kernel(
         for i in range(8):
             nc.tensor.transpose(warm[:, i % 4, :], x_raw[0][:, i % 4, 0:P], ident[:])
 
-        def quantize(name, grouped, width):
-            codes = sb.tile([P, width], U32, name=name + "_c", align_bytes=64)
+        def quantize(name, grouped, width, tag=None):
+            codes = sb.tile([P, width], U32, name=name + "_c", tag=tag or name + "_c", align_bytes=64)
             scales = sb.tile([P, width], U8, name=name + "_s", align_bytes=64)
             nc.vector.quantize_mx(out=codes[:].bitcast(FP8X4), scales=scales[:], in_=grouped)
             return codes, scales
@@ -138,15 +138,19 @@ def tile_list_mlat_qf_mask_kernel(
             for u in range(2):
                 nc.tensor.transpose(turned[:, u, :], pairs[:, u * P : (u + 1) * P], ident[:])
             qa_g[h, b] = sb.tile([P, P, PACK], BF16, name=f"qa_g{h}{b}", align_bytes=64)
-            nc.scalar.copy(out=qa_g[h, b][:].bitcast(F32), in_=turned[:].rearrange("p u m -> p m u"))
+            copy = nc.vector.tensor_copy if (h, b) == units[-1] else nc.scalar.copy
+            copy(out=qa_g[h, b][:].bitcast(F32), in_=turned[:].rearrange("p u m -> p m u"))
 
         picked_pairs = sb.tile([P, J], U32, name="picked_pairs", tag="x_g11", align_bytes=64)
         nc.vector.tensor_copy(picked_pairs[:], tab_w[:].bitcast(U32).indirect(offsets[:]))
         nc.vector.tensor_copy(out=picked_w[:], in_=picked_pairs[:].bitcast(U16).rearrange("p (j d) -> p d j", d=2))
 
-        wv8_g = sb.tile([P, N, PACK], BF16, name="wv8_g", tag="tab_w", align_bytes=64)
-        round_and_interleave(nc.vector.tensor_copy, wv8_g[:], wv8_raw[:])
-        wv8_c, wv8_s = quantize("wv8", wv8_g[:].rearrange("p n t -> p (n t)"), N)
+        wv8_tags = ("tab_w", "wv8_g1")
+        wv8_g = []
+        for g in range(2):
+            wv8_g.append(sb.tile([P, P, PACK], BF16, name=f"wv8_g{g}", tag=wv8_tags[g], align_bytes=64))
+            round_and_interleave(nc.vector.tensor_copy, wv8_g[g][:], wv8_raw[:, :, g * P : (g + 1) * P])
+        wv8_q = [quantize(f"wv8{g}", wv8_g[g][:].rearrange("p n t -> p (n t)"), P) for g in range(2)]
         for g in range(2):
             vv = ps.tile([P, J], F32, name=f"vv{g}", tag=f"bank{g}1")
             nc.tensor.matmul_mx(
@@ -160,8 +164,8 @@ def tile_list_mlat_qf_mask_kernel(
             )
             nc.tensor.matmul_mx(
                 out=vv[:],
-                lhsT=wv8_c[:, P * g : P * (g + 1)].bitcast(FP8X4),
-                lhsT_scale=wv8_s[:, P * g : P * (g + 1)],
+                lhsT=wv8_q[g][0][:].bitcast(FP8X4),
+                lhsT_scale=wv8_q[g][1][:],
                 rhs=picked_w[:, 0, :].bitcast(FP4X4),
                 rhs_scale=picked_s[:, 0, :],
                 start=False,
@@ -173,7 +177,8 @@ def tile_list_mlat_qf_mask_kernel(
 
         sc = [ps.tile([P, J], F32, name=f"sc{h}", tag=f"bank{h}0") for h in range(2)]
         for h, b in sorted(units):
-            codes, scales = quantize(f"qa{h}{b}", qa_g[h, b][:].rearrange("p m t -> p (m t)"), P)
+            tag = wv8_tags[h] if b == 0 else None
+            codes, scales = quantize(f"qa{h}{b}", qa_g[h, b][:].rearrange("p m t -> p (m t)"), P, tag=tag)
             nc.tensor.matmul_mx(
                 out=sc[h][:],
                 lhsT=codes[:].bitcast(FP8X4),

@@ -82,8 +82,6 @@ def tile_list_mlat_qf_mask_kernel(
         load_scale_rows(nc.sync, wv4_s, wv4_scales)
         nc.sync.dma_start(out=mask[:], in_=msk.rearrange("(h p) j -> p h j", p=P))
 
-        primer = sb.tile([P, 8], BF16, name="primer")
-        nc.scalar.copy(out=primer[:], in_=ident[:, 0:8])
         warm = ps.tile([P, 4, P], F32, name="warm", tag="turn11")
         for i in range(22):
             nc.tensor.transpose(warm[:, i % 4, :], ident[:], ident[:])

@@ -42,150 +42,174 @@ def tile_list_mlat_qf_mask_kernel(
     nc = tc.nc
     with ExitStack() as ctx:
         sb = ctx.enter_context(tc.tile_pool(name="sb", bufs=1))
+        ov = ctx.enter_context(tc.tile_pool(name="ov", bufs=1))
         ps = ctx.enter_context(tc.psum_pool(name="ps", bufs=1))
 
         offsets = sb.tile([P, J // 16], U16, name="offsets")
-        tab_s = sb.tile([P, 2, T], U8, name="tab_s", align_bytes=64)
+        tab_s = ov.tile([P, T], U8, name="tab_s", align_bytes=64, offset=5120)
         w4_s = sb.tile([P, 2, R], U8, name="w4_s", align_bytes=64)
         wv4_s = sb.tile([P, 1, N], U8, name="wv4_s", align_bytes=64)
-        x_raw = [sb.tile([P, PACK, M], F32, name=f"x_raw{a}") for a in range(2)]
-        w4_w = [sb.tile([P, 2, 2 * KP], U8, name=f"w4_w{b}", align_bytes=64) for b in range(2)]
-        tab_w = sb.tile([P, T], I32, name="tab_w", tag="tab_w", align_bytes=64)
-        wv8_raw = sb.tile([P, PACK, N], F32, name="wv8_raw")
+        plane0 = sb.tile([P, J], U8, name="plane0", align_bytes=64)
+        x_raw = [sb.tile([P, PACK, M], F32, name="x_raw0"), ov.tile([P, PACK, M], F32, name="x_raw1", align_bytes=64, offset=0)]
+        w4_w = [sb.tile([P, 2 * R], U8, name=f"w4_w{a}", align_bytes=64) for a in range(2)]
+        tab_w = sb.tile([P, T], I32, name="tab_w", align_bytes=64)
+        wv8_raw = ov.tile([P, PACK, N], F32, name="wv8_raw", align_bytes=64, offset=9216)
         wv4_w = sb.tile([P, 2 * N], U8, name="wv4_w", align_bytes=64)
-        mask = sb.tile([P, 2, J], F32, name="mask")
         ident = sb.tile([P, P], F32, name="ident")
 
-        nc.vector.memset(tab_s[:].bitcast(I32), 0)
         nc.vector.memset(w4_s[:].bitcast(I32), 0)
+        nc.vector.memset(tab_s[:].bitcast(I32), 0)
         nc.vector.memset(wv4_s[:].bitcast(I32), 0)
+        nc.vector.memset(plane0[:].bitcast(I32), 0)
         make_identity(nc, ident[:])
 
         def load_x(a):
             rows = x[a * KP : (a + 1) * KP, :].rearrange("(p t) m -> p t m", t=PACK)
             nc.sync.dma_start(out=x_raw[a][:], in_=rows)
 
-        def load_w4(b):
-            words = w4_words.rearrange("a p c -> p a c")[:, :, 2 * KP * b : 2 * KP * (b + 1)]
-            nc.sync.dma_start(out=w4_w[b][:].bitcast(I32), in_=words.bitcast(I32))
+        def load_w4(a):
+            nc.sync.dma_start(out=w4_w[a][:].bitcast(I32), in_=w4_words[a].bitcast(I32))
 
         nc.sync.dma_start(offsets[:], offs)
-        load_w4(0)
-        load_scale_rows(nc.sync, tab_s, tab_scales)
         load_x(0)
-        load_x(1)
         load_scale_rows(nc.sync, w4_s, w4_scales)
-        nc.sync.dma_start(out=tab_w[:], in_=tab_words[0].rearrange("p t b -> p (t b)").bitcast(I32))
+        load_w4(0)
+        load_x(1)
+        for q in range(1, 4):
+            nc.sync.dma_start(
+                out=tab_s[32 * q - 4 : 32 * q + 4, :].bitcast(I32), in_=tab_scales.bitcast(I32)[:, 4 * q : 4 * q + 4, :]
+            )
+        for a in range(2):
+            nc.sync.dma_start(out=tab_s[4 - 4 * a : 8 - 4 * a, :].bitcast(I32), in_=tab_scales.bitcast(I32)[a, 0:4, :])
         load_w4(1)
+        nc.sync.dma_start(out=tab_w[:], in_=tab_words[0].rearrange("p t b -> p (t b)").bitcast(I32))
+        load_scale_rows(nc.sync, wv4_s, wv4_scales)
         nc.sync.dma_start(out=wv8_raw[:], in_=wv8.rearrange("(p t) n -> p t n", t=PACK))
         nc.sync.dma_start(out=wv4_w[:].bitcast(I32), in_=wv4_words[0].bitcast(I32))
-        load_scale_rows(nc.sync, wv4_s, wv4_scales)
-        nc.sync.dma_start(out=mask[:], in_=msk.rearrange("(h p) j -> p h j", p=P))
 
-        warm = ps.tile([P, 4, P], F32, name="warm", tag="turn11")
-        for i in range(22):
-            nc.tensor.transpose(warm[:, i % 4, :], ident[:], ident[:])
-        for i in range(8):
-            nc.tensor.transpose(warm[:, i % 4, :], x_raw[0][:, i % 4, 0:P], ident[:])
-
-        def quantize(name, grouped, width, tag=None):
-            codes = sb.tile([P, width], U32, name=name + "_c", tag=tag or name + "_c", align_bytes=64)
+        def quantize(name, grouped, width, codes=None):
+            if codes is None:
+                codes = sb.tile([P, width], U32, name=name + "_c", align_bytes=64)
             scales = sb.tile([P, width], U8, name=name + "_s", align_bytes=64)
             nc.vector.quantize_mx(out=codes[:].bitcast(FP8X4), scales=scales[:], in_=grouped)
             return codes, scales
 
-        picked_s = sb.tile([P, 2, J], U8, name="picked_s", align_bytes=64)
-        picked_w = sb.tile([P, 2, J], U16, name="picked_w", align_bytes=64)
-
         x_q = {}
         for a in range(2):
+            grouped = [sb.tile([P, P, PACK], BF16, name=f"x_g{a}{h}", align_bytes=64) for h in range(2)]
+            round_and_interleave(nc.vector.tensor_copy, grouped[0][:], x_raw[a][:, :, 0:P])
+            round_and_interleave(nc.vector.tensor_copy, grouped[1][:, 0:64], x_raw[a][:, :, P : P + 64])
+            round_and_interleave(nc.scalar.copy, grouped[1][:, 64:P], x_raw[a][:, :, P + 64 : 2 * P])
             for h in range(2):
-                copy = nc.vector.tensor_copy if (a, h) == (1, 0) else nc.scalar.copy
-                grouped = sb.tile([P, P, PACK], BF16, name=f"x_g{a}{h}", tag=f"x_g{a * h}{h}", align_bytes=64)
-                round_and_interleave(copy, grouped[:], x_raw[a][:, :, h * P : (h + 1) * P])
-                x_q[a, h] = quantize(f"x{a}{h}", grouped[:].rearrange("p m t -> p (m t)"), P)
+                x_q[a, h] = quantize(f"x{a}{h}", grouped[h][:].rearrange("p m t -> p (m t)"), P)
 
-        for b in range(2):
-            nc.vector.tensor_copy(picked_s[:, b, :], tab_s[:, b, :].indirect(offsets[:]))
+        plane1 = ov.tile([P, J], U8, name="plane1", align_bytes=64, offset=0)
+        nc.vector.tensor_copy(plane1[:], tab_s[:].indirect(offsets[:]))
+        for lo, hi, shift in ((32, 96, -4), (96, 100, -4), (0, 4, 4)):
+            nc.sync.dma_start(out=plane0[lo:hi, :].bitcast(I32), in_=plane1[lo + shift : hi + shift, :].bitcast(I32))
+        planes = (plane0, plane1)
+        mask = ov.tile([P, 2, J], F32, name="mask", align_bytes=64, offset=5120)
+        nc.sync.dma_start(out=mask[:], in_=msk.rearrange("(h p) j -> p h j", p=P))
 
-        units = [(h, b) for b in range(2) for h in range(2)]
+        picked_pairs = ov.tile([P, J], U32, name="picked_pairs", align_bytes=64, offset=512)
+        for c in range(2):
+            nc.vector.tensor_copy(
+                picked_pairs[:, c * 256 : (c + 1) * 256], tab_w[:].bitcast(U32).indirect(offsets[:, c * 16 : (c + 1) * 16])
+            )
+        wv8_g = ov.tile([P, 2, P, PACK], BF16, name="wv8_g", align_bytes=64, offset=2560)
+        picked_w = sb.tile([P, 2, J], U16, name="picked_w", align_bytes=64)
+        for c in range(2):
+            nc.vector.tensor_copy(
+                out=picked_w[:, :, c * 256 : (c + 1) * 256],
+                in_=picked_pairs[:, c * 256 : (c + 1) * 256].bitcast(U16).rearrange("p (j d) -> p d j", d=2),
+            )
+        for g in range(2):
+            round_and_interleave(nc.vector.tensor_copy, wv8_g[:, g], wv8_raw[:, :, g * P : (g + 1) * P])
+
+        units = [(h, b) for h in range(2) for b in range(2)]
         qa_t = {}
         for h, b in units:
-            qa_t[h, b] = ps.tile([P, KP], F32, name=f"qa_t{h}{b}", tag=f"bank{h}{b}")
-        passes = [(h, 0, a) for a in range(2) for h in range(2)] + [(h, 1, a) for h in range(2) for a in range(2)]
-        for h, b, a in passes:
+            qa_t[h, b] = ps.tile([P, KP], F32, name=f"qa_t{h}{b}", tag=f"bank{(2 * h + b) % 3}")
+
+        def project(h, b, a, first):
             codes, scales = x_q[a, h]
             nc.tensor.matmul_mx(
                 out=qa_t[h, b][:],
                 lhsT=codes[:].bitcast(FP8X4),
                 lhsT_scale=scales[:],
-                rhs=w4_w[b][:, a, :].bitcast(FP4X4),
+                rhs=w4_w[a][:, 2 * KP * b : 2 * KP * (b + 1)].bitcast(FP4X4),
                 rhs_scale=w4_s[:, a, KP * b : KP * (b + 1)],
-                start=(a == 0),
-                stop=(a == 1),
+                start=first,
+                stop=not first,
             )
 
         rounded = {}
-        for h, b in units:
+        turned = [ps.tile([P, 2, 2, P], F32, name=f"turned{h}", tag=f"turn{h}") for h in range(2)]
+        qa_g = [sb.tile([P, 2, P, PACK], BF16, name=f"qa_g{h}", align_bytes=64) for h in range(2)]
+
+        def round_unit(h, b):
             rounded[h, b] = sb.tile([P, 2, P, 2], BF16, name=f"qa_r{h}{b}", align_bytes=64)
             nc.scalar.copy(out=rounded[h, b][:], in_=qa_t[h, b][:].rearrange("m (p u e) -> m u p e", u=2, e=2))
-        qa_g = {}
-        for h, b in units:
+
+        def turn(h, b):
             pairs = rounded[h, b][:].rearrange("m u p e -> m (u p e)").bitcast(F32)
-            turned = ps.tile([P, 2, P], F32, name=f"turned{h}{b}", tag=f"turn{h}{b}")
             for u in range(2):
-                nc.tensor.transpose(turned[:, u, :], pairs[:, u * P : (u + 1) * P], ident[:])
-            qa_g[h, b] = sb.tile([P, P, PACK], BF16, name=f"qa_g{h}{b}", align_bytes=64)
-            copy = nc.vector.tensor_copy if (h, b) == units[-1] else nc.scalar.copy
-            copy(out=qa_g[h, b][:].bitcast(F32), in_=turned[:].rearrange("p u m -> p m u"))
+                nc.tensor.transpose(turned[h][:, b, u, :], pairs[:, u * P : (u + 1) * P], ident[:])
 
-        picked_pairs = sb.tile([P, J], U32, name="picked_pairs", tag="x_g11", align_bytes=64)
-        nc.vector.tensor_copy(picked_pairs[:], tab_w[:].bitcast(U32).indirect(offsets[:]))
-        nc.vector.tensor_copy(out=picked_w[:], in_=picked_pairs[:].bitcast(U16).rearrange("p (j d) -> p d j", d=2))
+        for a in range(2):
+            for h, b in units[:3]:
+                project(h, b, a, a == 0)
+        for h, b in units[:3]:
+            round_unit(h, b)
+        for a in range(2):
+            project(1, 1, a, a == 0)
+        round_unit(1, 1)
+        for h, b in units:
+            turn(h, b)
+        for h in range(2):
+            nc.scalar.copy(out=qa_g[h][:].bitcast(F32), in_=turned[h][:].rearrange("p b u m -> p b m u"))
 
-        wv8_tags = ("tab_w", "wv8_g1")
-        wv8_g = []
+        vv = [ps.tile([P, J], F32, name=f"vv{g}", tag=("bank3", "bank1")[g]) for g in range(2)]
         for g in range(2):
-            wv8_g.append(sb.tile([P, P, PACK], BF16, name=f"wv8_g{g}", tag=wv8_tags[g], align_bytes=64))
-            round_and_interleave(nc.vector.tensor_copy, wv8_g[g][:], wv8_raw[:, :, g * P : (g + 1) * P])
-        wv8_q = [quantize(f"wv8{g}", wv8_g[g][:].rearrange("p n t -> p (n t)"), P) for g in range(2)]
-        for g in range(2):
-            vv = ps.tile([P, J], F32, name=f"vv{g}", tag=f"bank{g}1")
             nc.tensor.matmul_mx(
-                out=vv[:],
+                out=vv[g][:],
                 lhsT=wv4_w[:, 2 * P * g : 2 * P * (g + 1)].bitcast(FP4X4),
                 lhsT_scale=wv4_s[:, 0, P * g : P * (g + 1)],
                 rhs=picked_w[:, 1, :].bitcast(FP4X4),
-                rhs_scale=picked_s[:, 1, :],
+                rhs_scale=plane1[:],
                 start=True,
                 stop=False,
             )
+        sc = [ps.tile([P, J], F32, name=f"sc{h}") for h in range(2)]
+        for g in range(2):
+            codes, scales = quantize(f"wv8{g}", wv8_g[:, g].rearrange("p n t -> p (n t)"), P)
             nc.tensor.matmul_mx(
-                out=vv[:],
-                lhsT=wv8_q[g][0][:].bitcast(FP8X4),
-                lhsT_scale=wv8_q[g][1][:],
+                out=vv[g][:],
+                lhsT=codes[:].bitcast(FP8X4),
+                lhsT_scale=scales[:],
                 rhs=picked_w[:, 0, :].bitcast(FP4X4),
-                rhs_scale=picked_s[:, 0, :],
+                rhs_scale=plane0[:],
                 start=False,
                 stop=True,
             )
-            values = sb.tile([P, J], F32, name=f"values{g}")
-            nc.scalar.copy(out=values[:], in_=vv[:])
-            nc.sync.dma_start(out=out_1[g * P : (g + 1) * P, :], in_=values[:])
-
-        sc = [ps.tile([P, J], F32, name=f"sc{h}", tag=f"bank{h}0") for h in range(2)]
-        for h, b in sorted(units):
-            tag = wv8_tags[h] if b == 0 else None
-            codes, scales = quantize(f"qa{h}{b}", qa_g[h, b][:].rearrange("p m t -> p (m t)"), P, tag=tag)
-            nc.tensor.matmul_mx(
-                out=sc[h][:],
-                lhsT=codes[:].bitcast(FP8X4),
-                lhsT_scale=scales[:],
-                rhs=picked_w[:, b, :].bitcast(FP4X4),
-                rhs_scale=picked_s[:, b, :],
-                start=(b == 0),
-                stop=(b == 1),
-            )
+            for c in range(2):
+                cols = slice(c * J // 2, (c + 1) * J // 2)
+                values = sb.tile([P, J // 2], F32, name=f"values{g}{c}")
+                nc.scalar.copy(out=values[:], in_=vv[g][:, cols])
+                nc.sync.dma_start(out=out_1[g * P : (g + 1) * P, cols], in_=values[:])
+        for h in range(2):
+            codes = ov.tile([P, 2 * P], U32, name=f"qa{h}_c", align_bytes=64, offset=9216 + 1024 * h)
+            codes, scales = quantize(f"qa{h}", qa_g[h][:].rearrange("p b m t -> p (b m t)"), 2 * P, codes)
+            for b in range(2):
+                nc.tensor.matmul_mx(
+                    out=sc[h][:],
+                    lhsT=codes[:, b * P : (b + 1) * P].bitcast(FP8X4),
+                    lhsT_scale=scales[:, b * P : (b + 1) * P],
+                    rhs=picked_w[:, b, :].bitcast(FP4X4),
+                    rhs_scale=planes[b][:],
+                    start=(b == 0),
+                    stop=(b == 1),
+                )
         for h in range(2):
             for c in range(2):
                 cols = slice(c * J // 2, (c + 1) * J // 2)

@@ -46,14 +46,14 @@ def tile_list_mlat_qf_mask_kernel(
         ps = ctx.enter_context(tc.psum_pool(name="ps", bufs=1))
 
         offsets = sb.tile([P, J // 16], U16, name="offsets")
-        tab_s = ov.tile([P, T], U8, name="tab_s", align_bytes=64, offset=5120)
+        tab_s = ov.tile([P, T], U8, name="tab_s", align_bytes=64, offset=7168)
         w4_s = sb.tile([P, 2, R], U8, name="w4_s", align_bytes=64)
         wv4_s = sb.tile([P, 1, N], U8, name="wv4_s", align_bytes=64)
         plane0 = sb.tile([P, J], U8, name="plane0", align_bytes=64)
         x_raw = [sb.tile([P, PACK, M], F32, name="x_raw0"), ov.tile([P, PACK, M], F32, name="x_raw1", align_bytes=64, offset=0)]
         w4_w = [sb.tile([P, 2 * R], U8, name=f"w4_w{a}", align_bytes=64) for a in range(2)]
         tab_w = sb.tile([P, T], I32, name="tab_w", align_bytes=64)
-        wv8_raw = ov.tile([P, PACK, N], F32, name="wv8_raw", align_bytes=64, offset=9216)
+        wv8_raw = ov.tile([P, PACK, N], F32, name="wv8_raw", align_bytes=64, offset=10240)
         wv4_w = sb.tile([P, 2 * N], U8, name="wv4_w", align_bytes=64)
         ident = sb.tile([P, P], F32, name="ident")
 
@@ -75,13 +75,11 @@ def tile_list_mlat_qf_mask_kernel(
         load_scale_rows(nc.sync, w4_s, w4_scales)
         load_w4(0)
         load_x(1)
-        for q in range(1, 4):
-            nc.sync.dma_start(
-                out=tab_s[32 * q - 4 : 32 * q + 4, :].bitcast(I32), in_=tab_scales.bitcast(I32)[:, 4 * q : 4 * q + 4, :]
-            )
-        for a in range(2):
-            nc.sync.dma_start(out=tab_s[4 - 4 * a : 8 - 4 * a, :].bitcast(I32), in_=tab_scales.bitcast(I32)[a, 0:4, :])
         load_w4(1)
+        rows = tab_scales.bitcast(I32)
+        nc.sync.dma_start(out=tab_s[8:24, :].bitcast(I32), in_=rows[0])
+        for r in range(4):
+            nc.sync.dma_start(out=tab_s[r:P:32, :].bitcast(I32), in_=rows[1].rearrange("(q r) n -> r q n", r=4)[r])
         nc.sync.dma_start(out=tab_w[:], in_=tab_words[0].rearrange("p t b -> p (t b)").bitcast(I32))
         load_scale_rows(nc.sync, wv4_s, wv4_scales)
         nc.sync.dma_start(out=wv8_raw[:], in_=wv8.rearrange("(p t) n -> p t n", t=PACK))
@@ -105,11 +103,13 @@ def tile_list_mlat_qf_mask_kernel(
 
         plane1 = ov.tile([P, J], U8, name="plane1", align_bytes=64, offset=0)
         nc.vector.tensor_copy(plane1[:], tab_s[:].indirect(offsets[:]))
-        for lo, hi, shift in ((32, 96, -4), (96, 100, -4), (0, 4, 4)):
-            nc.sync.dma_start(out=plane0[lo:hi, :].bitcast(I32), in_=plane1[lo + shift : hi + shift, :].bitcast(I32))
+        for r in range(4):
+            nc.sync.dma_start(out=plane0[r:P:32, :].bitcast(I32), in_=plane1[8 + r : 24 : 4, :].bitcast(I32))
         planes = (plane0, plane1)
-        mask = ov.tile([P, 2, J], F32, name="mask", align_bytes=64, offset=5120)
-        nc.sync.dma_start(out=mask[:], in_=msk.rearrange("(h p) j -> p h j", p=P))
+        mask = []
+        for h in range(2):
+            mask.append(ov.tile([P, J], F32, name=f"mask{h}", align_bytes=64, offset=5632 + 2048 * h))
+            nc.sync.dma_start(out=mask[h][:], in_=msk[h * P : (h + 1) * P, :])
 
         picked_pairs = ov.tile([P, J], U32, name="picked_pairs", align_bytes=64, offset=512)
         for c in range(2):
@@ -198,7 +198,7 @@ def tile_list_mlat_qf_mask_kernel(
                 nc.scalar.copy(out=values[:], in_=vv[g][:, cols])
                 nc.sync.dma_start(out=out_1[g * P : (g + 1) * P, cols], in_=values[:])
         for h in range(2):
-            codes = ov.tile([P, 2 * P], U32, name=f"qa{h}_c", align_bytes=64, offset=9216 + 1024 * h)
+            codes = ov.tile([P, 2 * P], U32, name=f"qa{h}_c", align_bytes=64, offset=10240 + 1024 * h)
             codes, scales = quantize(f"qa{h}", qa_g[h][:].rearrange("p b m t -> p (b m t)"), 2 * P, codes)
             for b in range(2):
                 nc.tensor.matmul_mx(
@@ -215,6 +215,6 @@ def tile_list_mlat_qf_mask_kernel(
                 cols = slice(c * J // 2, (c + 1) * J // 2)
                 scores = sb.tile([P, J // 2], F32, name=f"scores{h}{c}")
                 nc.vector.scalar_tensor_tensor(
-                    out=scores[:], in0=sc[h][:, cols], scalar=SCORE_SCALE, in1=mask[:, h, cols], op0=MULT, op1=ADD
+                    out=scores[:], in0=sc[h][:, cols], scalar=SCORE_SCALE, in1=mask[h][:, cols], op0=MULT, op1=ADD
                 )
                 nc.sync.dma_start(out=out_0[h * P : (h + 1) * P, cols], in_=scores[:])

@@ -46,11 +46,11 @@ def tile_list_mlat_qf_mask_kernel(
         ps = ctx.enter_context(tc.psum_pool(name="ps", bufs=1))
 
         offsets = sb.tile([P, J // 16], U16, name="offsets")
-        tab_s = ov.tile([P, T], U8, name="tab_s", align_bytes=64, offset=7168)
+        tab_s = sb.tile([P, T], U8, name="tab_s", align_bytes=64)
         w4_s = sb.tile([P, 2, R], U8, name="w4_s", align_bytes=64)
-        wv4_s = sb.tile([P, 1, N], U8, name="wv4_s", align_bytes=64)
-        plane0 = sb.tile([P, J], U8, name="plane0", align_bytes=64)
-        x_raw = [sb.tile([P, PACK, M], F32, name="x_raw0"), ov.tile([P, PACK, M], F32, name="x_raw1", align_bytes=64, offset=0)]
+        planes = sb.tile([P, 2 * J + N], U8, name="planes", align_bytes=64)
+        staged = ov.tile([P, J + N], U8, name="staged", align_bytes=64, offset=5120)
+        x_raw = [ov.tile([P, PACK, M], F32, name="x_raw0", align_bytes=64, offset=5120), ov.tile([P, PACK, M], F32, name="x_raw1", align_bytes=64, offset=0)]
         w4_w = [sb.tile([P, 2 * R], U8, name=f"w4_w{a}", align_bytes=64) for a in range(2)]
         tab_w = sb.tile([P, T], I32, name="tab_w", align_bytes=64)
         wv8_raw = ov.tile([P, PACK, N], F32, name="wv8_raw", align_bytes=64, offset=10240)
@@ -58,9 +58,8 @@ def tile_list_mlat_qf_mask_kernel(
         ident = sb.tile([P, P], F32, name="ident")
 
         nc.vector.memset(w4_s[:].bitcast(I32), 0)
-        nc.vector.memset(tab_s[:].bitcast(I32), 0)
-        nc.vector.memset(wv4_s[:].bitcast(I32), 0)
-        nc.vector.memset(plane0[:].bitcast(I32), 0)
+        nc.vector.memset(tab_s[0:96, :].bitcast(I32), 0)
+        nc.vector.memset(planes[:].bitcast(I32), 0)
         make_identity(nc, ident[:])
 
         def load_x(a):
@@ -71,19 +70,15 @@ def tile_list_mlat_qf_mask_kernel(
             nc.sync.dma_start(out=w4_w[a][:].bitcast(I32), in_=w4_words[a].bitcast(I32))
 
         nc.sync.dma_start(offsets[:], offs)
+        nc.scalar.dma_start(out=tab_s[96:P, :].bitcast(I32), in_=tab_scales.bitcast(I32).rearrange("a q n -> (a q) n"))
         load_x(0)
         load_scale_rows(nc.sync, w4_s, w4_scales)
         load_w4(0)
         load_x(1)
         load_w4(1)
-        rows = tab_scales.bitcast(I32)
-        nc.sync.dma_start(out=tab_s[8:24, :].bitcast(I32), in_=rows[0])
-        for r in range(4):
-            nc.sync.dma_start(out=tab_s[r:P:32, :].bitcast(I32), in_=rows[1].rearrange("(q r) n -> r q n", r=4)[r])
         nc.sync.dma_start(out=tab_w[:], in_=tab_words[0].rearrange("p t b -> p (t b)").bitcast(I32))
-        load_scale_rows(nc.sync, wv4_s, wv4_scales)
-        nc.sync.dma_start(out=wv8_raw[:], in_=wv8.rearrange("(p t) n -> p t n", t=PACK))
-        nc.sync.dma_start(out=wv4_w[:].bitcast(I32), in_=wv4_words[0].bitcast(I32))
+        picked_s = sb.tile([P, J], U8, name="picked_s", align_bytes=64)
+        nc.vector.tensor_copy(picked_s[:], tab_s[:].indirect(offsets[:]))
 
         def quantize(name, grouped, width, codes=None):
             if codes is None:
@@ -93,23 +88,35 @@ def tile_list_mlat_qf_mask_kernel(
             return codes, scales
 
         x_q = {}
-        for a in range(2):
+
+        def quantize_x(a, split):
             grouped = [sb.tile([P, P, PACK], BF16, name=f"x_g{a}{h}", align_bytes=64) for h in range(2)]
             round_and_interleave(nc.vector.tensor_copy, grouped[0][:], x_raw[a][:, :, 0:P])
-            round_and_interleave(nc.vector.tensor_copy, grouped[1][:, 0:64], x_raw[a][:, :, P : P + 64])
-            round_and_interleave(nc.scalar.copy, grouped[1][:, 64:P], x_raw[a][:, :, P + 64 : 2 * P])
+            if split:
+                round_and_interleave(nc.vector.tensor_copy, grouped[1][:, 0:split], x_raw[a][:, :, P : P + split])
+            round_and_interleave(nc.scalar.copy, grouped[1][:, split:P], x_raw[a][:, :, P + split : 2 * P])
             for h in range(2):
                 x_q[a, h] = quantize(f"x{a}{h}", grouped[h][:].rearrange("p m t -> p (m t)"), P)
 
-        plane1 = ov.tile([P, J], U8, name="plane1", align_bytes=64, offset=0)
-        nc.vector.tensor_copy(plane1[:], tab_s[:].indirect(offsets[:]))
+        quantize_x(0, 0)
+        nc.vector.tensor_copy(staged[:, 0:J].bitcast(I32), picked_s[:].bitcast(I32))
+        nc.sync.dma_start(out=staged[112:P, J : J + N].bitcast(I32), in_=wv4_scales.bitcast(I32)[0])
+
+        def move0(r):
+            nc.sync.dma_start(out=planes[r:P:32, 0:J].bitcast(I32), in_=picked_s[96 + r : 112 : 4, :].bitcast(I32))
+
         for r in range(4):
-            nc.sync.dma_start(out=plane0[r:P:32, :].bitcast(I32), in_=plane1[8 + r : 24 : 4, :].bitcast(I32))
-        planes = (plane0, plane1)
+            move0(r)
+        nc.sync.dma_start(out=wv8_raw[:], in_=wv8.rearrange("(p t) n -> p t n", t=PACK))
+        nc.sync.dma_start(out=wv4_w[:].bitcast(I32), in_=wv4_words[0].bitcast(I32))
+        for r in range(4):
+            nc.sync.dma_start(out=planes[r:P:32, J:].bitcast(I32), in_=staged[112 + r : P : 4, :].bitcast(I32))
         mask = []
         for h in range(2):
-            mask.append(ov.tile([P, J], F32, name=f"mask{h}", align_bytes=64, offset=5632 + 2048 * h))
+            mask.append(sb.tile([P, J], F32, name=f"mask{h}", align_bytes=64))
             nc.sync.dma_start(out=mask[h][:], in_=msk[h * P : (h + 1) * P, :])
+
+        quantize_x(1, 64)
 
         picked_pairs = ov.tile([P, J], U32, name="picked_pairs", align_bytes=64, offset=512)
         for c in range(2):
@@ -174,9 +181,9 @@ def tile_list_mlat_qf_mask_kernel(
             nc.tensor.matmul_mx(
                 out=vv[g][:],
                 lhsT=wv4_w[:, 2 * P * g : 2 * P * (g + 1)].bitcast(FP4X4),
-                lhsT_scale=wv4_s[:, 0, P * g : P * (g + 1)],
+                lhsT_scale=planes[:, 2 * J + P * g : 2 * J + P * (g + 1)],
                 rhs=picked_w[:, 1, :].bitcast(FP4X4),
-                rhs_scale=plane1[:],
+                rhs_scale=planes[:, J : 2 * J],
                 start=True,
                 stop=False,
             )
@@ -188,7 +195,7 @@ def tile_list_mlat_qf_mask_kernel(
                 lhsT=codes[:].bitcast(FP8X4),
                 lhsT_scale=scales[:],
                 rhs=picked_w[:, 0, :].bitcast(FP4X4),
-                rhs_scale=plane0[:],
+                rhs_scale=planes[:, 0:J],
                 start=False,
                 stop=True,
             )
@@ -200,15 +207,15 @@ def tile_list_mlat_qf_mask_kernel(
         for h in range(2):
             codes = ov.tile([P, 2 * P], U32, name=f"qa{h}_c", align_bytes=64, offset=10240 + 1024 * h)
             codes, scales = quantize(f"qa{h}", qa_g[h][:].rearrange("p b m t -> p (b m t)"), 2 * P, codes)
-            for b in range(2):
+            for b in (1, 0):
                 nc.tensor.matmul_mx(
                     out=sc[h][:],
                     lhsT=codes[:, b * P : (b + 1) * P].bitcast(FP8X4),
                     lhsT_scale=scales[:, b * P : (b + 1) * P],
                     rhs=picked_w[:, b, :].bitcast(FP4X4),
-                    rhs_scale=planes[b][:],
-                    start=(b == 0),
-                    stop=(b == 1),
+                    rhs_scale=planes[:, b * J : (b + 1) * J],
+                    start=(b == 1),
+                    stop=(b == 0),
                 )
         for h in range(2):
             for c in range(2):

@@ -98,7 +98,15 @@ def tile_list_mlat_qf_mask_kernel(
             for h in range(2):
                 x_q[a, h] = quantize(f"x{a}{h}", grouped[h][:].rearrange("p m t -> p (m t)"), P)
 
+        def deal(out, in_):
+            nc.vector.tensor_copy(out=out.rearrange("p (t m) -> p t m", t=PACK), in_=in_.rearrange("p (m t) -> p t m", t=PACK))
+
+        w4_dw = [sb.tile([P, KP], U16, name=f"w4_dw{a}", align_bytes=64) for a in range(2)]
+        w4_ds = [sb.tile([P, KP], U8, name=f"w4_ds{a}", align_bytes=64) for a in range(2)]
         quantize_x(0, 0)
+        for a in range(2):
+            deal(w4_ds[a][:], w4_s[:, a, KP:R])
+        deal(w4_dw[0][:], w4_w[0][:].bitcast(U16)[:, KP:R])
         nc.vector.tensor_copy(staged[:, 0:J].bitcast(I32), picked_s[:].bitcast(I32))
         nc.sync.dma_start(out=staged[112:P, J : J + N].bitcast(I32), in_=wv4_scales.bitcast(I32)[0])
 
@@ -117,6 +125,7 @@ def tile_list_mlat_qf_mask_kernel(
             nc.sync.dma_start(out=mask[h][:], in_=msk[h * P : (h + 1) * P, :])
 
         quantize_x(1, 64)
+        deal(w4_dw[1][:], w4_w[1][:].bitcast(U16)[:, KP:R])
 
         picked_pairs = ov.tile([P, J], U32, name="picked_pairs", align_bytes=64, offset=512)
         for c in range(2):
@@ -133,50 +142,45 @@ def tile_list_mlat_qf_mask_kernel(
         for g in range(2):
             round_and_interleave(nc.vector.tensor_copy, wv8_g[:, g], wv8_raw[:, :, g * P : (g + 1) * P])
 
-        units = [(h, b) for h in range(2) for b in range(2)]
-        qa_t = {}
-        for h, b in units:
-            qa_t[h, b] = ps.tile([P, KP], F32, name=f"qa_t{h}{b}", tag=f"bank{(2 * h + b) % 3}")
-
-        def project(h, b, a, first):
-            codes, scales = x_q[a, h]
-            nc.tensor.matmul_mx(
-                out=qa_t[h, b][:],
-                lhsT=codes[:].bitcast(FP8X4),
-                lhsT_scale=scales[:],
-                rhs=w4_w[a][:, 2 * KP * b : 2 * KP * (b + 1)].bitcast(FP4X4),
-                rhs_scale=w4_s[:, a, KP * b : KP * (b + 1)],
-                start=first,
-                stop=not first,
-            )
-
-        rounded = {}
-        turned = [ps.tile([P, 2, 2, P], F32, name=f"turned{h}", tag=f"turn{h}") for h in range(2)]
+        direct = [ps.tile([P, KP], F32, name=f"direct{h}", tag=f"bank{h}") for h in range(2)]
+        dealt = [ps.tile([P, PACK, P], F32, name=f"dealt{h}") for h in range(2)]
+        turned = [ps.tile([P, 2, P], F32, name=f"turned{h}") for h in range(2)]
         qa_g = [sb.tile([P, 2, P, PACK], BF16, name=f"qa_g{h}", align_bytes=64) for h in range(2)]
-
-        def round_unit(h, b):
-            rounded[h, b] = sb.tile([P, 2, P, 2], BF16, name=f"qa_r{h}{b}", align_bytes=64)
-            nc.scalar.copy(out=rounded[h, b][:], in_=qa_t[h, b][:].rearrange("m (p u e) -> m u p e", u=2, e=2))
-
-        def turn(h, b):
-            pairs = rounded[h, b][:].rearrange("m u p e -> m (u p e)").bitcast(F32)
-            for u in range(2):
-                nc.tensor.transpose(turned[h][:, b, u, :], pairs[:, u * P : (u + 1) * P], ident[:])
-
         for a in range(2):
-            for h, b in units[:3]:
-                project(h, b, a, a == 0)
-        for h, b in units[:3]:
-            round_unit(h, b)
-        for a in range(2):
-            project(1, 1, a, a == 0)
-        round_unit(1, 1)
-        for h, b in units:
-            turn(h, b)
+            for h in range(2):
+                codes, scales = x_q[a, h]
+                nc.tensor.matmul_mx(
+                    out=direct[h][:],
+                    lhsT=codes[:].bitcast(FP8X4),
+                    lhsT_scale=scales[:],
+                    rhs=w4_w[a][:, 0 : 2 * KP].bitcast(FP4X4),
+                    rhs_scale=w4_s[:, a, 0:KP],
+                    start=(a == 0),
+                    stop=(a == 1),
+                )
+            for h in range(2):
+                codes, scales = x_q[a, h]
+                for t in range(PACK):
+                    nc.tensor.matmul_mx(
+                        out=dealt[h][:, t, :],
+                        lhsT=w4_dw[a][:, P * t : P * (t + 1)].bitcast(FP4X4),
+                        lhsT_scale=w4_ds[a][:, P * t : P * (t + 1)],
+                        rhs=codes[:].bitcast(FP8X4),
+                        rhs_scale=scales[:],
+                        start=(a == 0 and t == 0),
+                        stop=(a == 1 and t == PACK - 1),
+                    )
         for h in range(2):
-            nc.scalar.copy(out=qa_g[h][:].bitcast(F32), in_=turned[h][:].rearrange("p b u m -> p b m u"))
+            rounded = sb.tile([P, 2, P, 2], BF16, name=f"qa_r{h}", align_bytes=64)
+            nc.scalar.copy(out=rounded[:], in_=direct[h][:].rearrange("m (p u e) -> m u p e", u=2, e=2))
+            pairs = rounded[:].rearrange("m u p e -> m (u p e)").bitcast(F32)
+            for u in range(2):
+                nc.tensor.transpose(turned[h][:, u, :], pairs[:, u * P : (u + 1) * P], ident[:])
+        for h in range(2):
+            nc.scalar.copy(out=qa_g[h][:, 1], in_=dealt[h][:].rearrange("p t m -> p m t"))
+            nc.scalar.copy(out=qa_g[h][:, 0].bitcast(F32), in_=turned[h][:].rearrange("p u m -> p m u"))
 
-        vv = [ps.tile([P, J], F32, name=f"vv{g}", tag=("bank3", "bank1")[g]) for g in range(2)]
+        vv = [ps.tile([P, J], F32, name=f"vv{g}", tag=f"bank{g}") for g in range(2)]
         for g in range(2):
             nc.tensor.matmul_mx(
                 out=vv[g][:],

@@ -49,8 +49,8 @@ def tile_list_mlat_qf_mask_kernel(
         tab_s = sb.tile([P, T], U8, name="tab_s", align_bytes=64)
         w4_s = sb.tile([P, 2, R], U8, name="w4_s", align_bytes=64)
         planes = sb.tile([P, 2 * J + N], U8, name="planes", align_bytes=64)
-        staged = ov.tile([P, J + N], U8, name="staged", align_bytes=64, offset=5120)
-        x_raw = [ov.tile([P, PACK, M], F32, name="x_raw0", align_bytes=64, offset=5120), ov.tile([P, PACK, M], F32, name="x_raw1", align_bytes=64, offset=0)]
+        staged = ov.tile([P, J + N], U8, name="staged", align_bytes=64, offset=512)
+        x_raw = [sb.tile([P, PACK, M], F32, name="x_raw0"), ov.tile([P, PACK, M], F32, name="x_raw1", align_bytes=64, offset=0)]
         w4_w = [sb.tile([P, 2 * R], U8, name=f"w4_w{a}", align_bytes=64) for a in range(2)]
         tab_w = sb.tile([P, T], I32, name="tab_w", align_bytes=64)
         wv8_raw = ov.tile([P, PACK, N], F32, name="wv8_raw", align_bytes=64, offset=10240)
@@ -75,6 +75,7 @@ def tile_list_mlat_qf_mask_kernel(
         load_scale_rows(nc.sync, w4_s, w4_scales)
         load_w4(0)
         load_x(1)
+        nc.sync.dma_start(out=planes[112:P, 2 * J :].bitcast(I32), in_=wv4_scales.bitcast(I32)[0])
         load_w4(1)
         nc.sync.dma_start(out=tab_w[:], in_=tab_words[0].rearrange("p t b -> p (t b)").bitcast(I32))
         picked_s = sb.tile([P, J], U8, name="picked_s", align_bytes=64)
@@ -102,37 +103,42 @@ def tile_list_mlat_qf_mask_kernel(
             nc.vector.tensor_copy(out=out.rearrange("p (t m) -> p t m", t=PACK), in_=in_.rearrange("p (m t) -> p t m", t=PACK))
 
         w4_dw = [sb.tile([P, KP], U16, name=f"w4_dw{a}", align_bytes=64) for a in range(2)]
-        w4_ds = [sb.tile([P, KP], U8, name=f"w4_ds{a}", align_bytes=64) for a in range(2)]
+        w4_ds = [sb.tile([P, KP], U8, name="w4_ds0", align_bytes=64), ov.tile([P, KP], U8, name="w4_ds1", align_bytes=64, offset=0)]
         quantize_x(0, 0)
-        for a in range(2):
-            deal(w4_ds[a][:], w4_s[:, a, KP:R])
+        deal(w4_ds[0][:], w4_s[:, 0, KP:R])
         deal(w4_dw[0][:], w4_w[0][:].bitcast(U16)[:, KP:R])
+        quantize_x(1, 64)
         nc.vector.tensor_copy(staged[:, 0:J].bitcast(I32), picked_s[:].bitcast(I32))
-        nc.sync.dma_start(out=staged[112:P, J : J + N].bitcast(I32), in_=wv4_scales.bitcast(I32)[0])
+        nc.vector.tensor_copy(staged[:, J:].bitcast(I32), planes[:, 2 * J :].bitcast(I32))
 
-        def move0(r):
-            nc.sync.dma_start(out=planes[r:P:32, 0:J].bitcast(I32), in_=picked_s[96 + r : 112 : 4, :].bitcast(I32))
+        def move(a, r):
+            if a == 0:
+                nc.sync.dma_start(out=planes[r:P:32, 0:J].bitcast(I32), in_=picked_s[96 + r : 112 : 4, :].bitcast(I32))
+            else:
+                nc.sync.dma_start(out=planes[r:P:32, J:].bitcast(I32), in_=staged[112 + r : P : 4, :].bitcast(I32))
 
-        for r in range(4):
-            move0(r)
+        for r in range(2):
+            move(0, r)
         nc.sync.dma_start(out=wv8_raw[:], in_=wv8.rearrange("(p t) n -> p t n", t=PACK))
         nc.sync.dma_start(out=wv4_w[:].bitcast(I32), in_=wv4_words[0].bitcast(I32))
         for r in range(4):
-            nc.sync.dma_start(out=planes[r:P:32, J:].bitcast(I32), in_=staged[112 + r : P : 4, :].bitcast(I32))
+            move(1, r)
+        for r in range(2, 4):
+            move(0, r)
         mask = []
         for h in range(2):
             mask.append(sb.tile([P, J], F32, name=f"mask{h}", align_bytes=64))
             nc.sync.dma_start(out=mask[h][:], in_=msk[h * P : (h + 1) * P, :])
 
-        quantize_x(1, 64)
+        deal(w4_ds[1][:], w4_s[:, 1, KP:R])
         deal(w4_dw[1][:], w4_w[1][:].bitcast(U16)[:, KP:R])
 
-        picked_pairs = ov.tile([P, J], U32, name="picked_pairs", align_bytes=64, offset=512)
+        picked_pairs = ov.tile([P, J], U32, name="picked_pairs", align_bytes=64, offset=1280)
         for c in range(2):
             nc.vector.tensor_copy(
                 picked_pairs[:, c * 256 : (c + 1) * 256], tab_w[:].bitcast(U32).indirect(offsets[:, c * 16 : (c + 1) * 16])
             )
-        wv8_g = ov.tile([P, 2, P, PACK], BF16, name="wv8_g", align_bytes=64, offset=2560)
+        wv8_g = sb.tile([P, 2, P, PACK], BF16, name="wv8_g", align_bytes=64)
         picked_w = sb.tile([P, 2, J], U16, name="picked_w", align_bytes=64)
         for c in range(2):
             nc.vector.tensor_copy(
@@ -143,44 +149,53 @@ def tile_list_mlat_qf_mask_kernel(
             round_and_interleave(nc.vector.tensor_copy, wv8_g[:, g], wv8_raw[:, :, g * P : (g + 1) * P])
 
         direct = [ps.tile([P, KP], F32, name=f"direct{h}", tag=f"bank{h}") for h in range(2)]
-        dealt = [ps.tile([P, PACK, P], F32, name=f"dealt{h}") for h in range(2)]
+        dealt = [ps.tile([P, PACK, P], F32, name=f"dealt{h}", tag=("bank2", "bank0")[h]) for h in range(2)]
         turned = [ps.tile([P, 2, P], F32, name=f"turned{h}") for h in range(2)]
         qa_g = [sb.tile([P, 2, P, PACK], BF16, name=f"qa_g{h}", align_bytes=64) for h in range(2)]
+
+        def project_direct(a, h):
+            codes, scales = x_q[a, h]
+            nc.tensor.matmul_mx(
+                out=direct[h][:],
+                lhsT=codes[:].bitcast(FP8X4),
+                lhsT_scale=scales[:],
+                rhs=w4_w[a][:, 0 : 2 * KP].bitcast(FP4X4),
+                rhs_scale=w4_s[:, a, 0:KP],
+                start=(a == 0),
+                stop=(a == 1),
+            )
+
+        def project_dealt(a, h):
+            codes, scales = x_q[a, h]
+            for t in range(PACK):
+                nc.tensor.matmul_mx(
+                    out=dealt[h][:, t, :],
+                    lhsT=w4_dw[a][:, P * t : P * (t + 1)].bitcast(FP4X4),
+                    lhsT_scale=w4_ds[a][:, P * t : P * (t + 1)],
+                    rhs=codes[:].bitcast(FP8X4),
+                    rhs_scale=scales[:],
+                    start=(a == 0 and t == 0),
+                    stop=(a == 1 and t == PACK - 1),
+                )
+
         for a in range(2):
             for h in range(2):
-                codes, scales = x_q[a, h]
-                nc.tensor.matmul_mx(
-                    out=direct[h][:],
-                    lhsT=codes[:].bitcast(FP8X4),
-                    lhsT_scale=scales[:],
-                    rhs=w4_w[a][:, 0 : 2 * KP].bitcast(FP4X4),
-                    rhs_scale=w4_s[:, a, 0:KP],
-                    start=(a == 0),
-                    stop=(a == 1),
-                )
-            for h in range(2):
-                codes, scales = x_q[a, h]
-                for t in range(PACK):
-                    nc.tensor.matmul_mx(
-                        out=dealt[h][:, t, :],
-                        lhsT=w4_dw[a][:, P * t : P * (t + 1)].bitcast(FP4X4),
-                        lhsT_scale=w4_ds[a][:, P * t : P * (t + 1)],
-                        rhs=codes[:].bitcast(FP8X4),
-                        rhs_scale=scales[:],
-                        start=(a == 0 and t == 0),
-                        stop=(a == 1 and t == PACK - 1),
-                    )
+                project_direct(a, h)
+            project_dealt(a, 0)
+        rounded = [sb.tile([P, 2, P, 2], BF16, name=f"qa_r{h}", align_bytes=64) for h in range(2)]
         for h in range(2):
-            rounded = sb.tile([P, 2, P, 2], BF16, name=f"qa_r{h}", align_bytes=64)
-            nc.scalar.copy(out=rounded[:], in_=direct[h][:].rearrange("m (p u e) -> m u p e", u=2, e=2))
-            pairs = rounded[:].rearrange("m u p e -> m (u p e)").bitcast(F32)
+            nc.scalar.copy(out=rounded[h][:], in_=direct[h][:].rearrange("m (p u e) -> m u p e", u=2, e=2))
+        for a in range(2):
+            project_dealt(a, 1)
+        for h in range(2):
+            pairs = rounded[h][:].rearrange("m u p e -> m (u p e)").bitcast(F32)
             for u in range(2):
                 nc.tensor.transpose(turned[h][:, u, :], pairs[:, u * P : (u + 1) * P], ident[:])
         for h in range(2):
             nc.scalar.copy(out=qa_g[h][:, 1], in_=dealt[h][:].rearrange("p t m -> p m t"))
             nc.scalar.copy(out=qa_g[h][:, 0].bitcast(F32), in_=turned[h][:].rearrange("p u m -> p m u"))
 
-        vv = [ps.tile([P, J], F32, name=f"vv{g}", tag=f"bank{g}") for g in range(2)]
+        vv = [ps.tile([P, J], F32, name=f"vv{g}", tag=("bank3", "bank1")[g]) for g in range(2)]
         for g in range(2):
             nc.tensor.matmul_mx(
                 out=vv[g][:],

@@ -49,8 +49,8 @@ def tile_list_mlat_qf_mask_kernel(
         tab_s = sb.tile([P, T], U8, name="tab_s", align_bytes=64)
         w4_s = sb.tile([P, 2, R], U8, name="w4_s", align_bytes=64)
         planes = sb.tile([P, 2 * J + N], U8, name="planes", align_bytes=64)
-        staged = ov.tile([P, J + N], U8, name="staged", align_bytes=64, offset=512)
-        x_raw = [sb.tile([P, PACK, M], F32, name="x_raw0"), ov.tile([P, PACK, M], F32, name="x_raw1", align_bytes=64, offset=0)]
+        staged = ov.tile([P, J + N], U8, name="staged", align_bytes=64, offset=5120)
+        x_raw = [ov.tile([P, PACK, M], F32, name="x_raw0", align_bytes=64, offset=5120), ov.tile([P, PACK, M], F32, name="x_raw1", align_bytes=64, offset=0)]
         w4_w = [sb.tile([P, 2 * R], U8, name=f"w4_w{a}", align_bytes=64) for a in range(2)]
         tab_w = sb.tile([P, T], I32, name="tab_w", align_bytes=64)
         wv8_raw = ov.tile([P, PACK, N], F32, name="wv8_raw", align_bytes=64, offset=10240)
@@ -103,13 +103,20 @@ def tile_list_mlat_qf_mask_kernel(
             nc.vector.tensor_copy(out=out.rearrange("p (t m) -> p t m", t=PACK), in_=in_.rearrange("p (m t) -> p t m", t=PACK))
 
         w4_dw = [sb.tile([P, KP], U16, name=f"w4_dw{a}", align_bytes=64) for a in range(2)]
-        w4_ds = [sb.tile([P, KP], U8, name="w4_ds0", align_bytes=64), ov.tile([P, KP], U8, name="w4_ds1", align_bytes=64, offset=0)]
+        w4_ds = [sb.tile([P, KP], U8, name="w4_ds0", align_bytes=64), sb.tile([P, KP], U8, name="w4_ds1", align_bytes=64)]
         quantize_x(0, 0)
-        deal(w4_ds[0][:], w4_s[:, 0, KP:R])
-        deal(w4_dw[0][:], w4_w[0][:].bitcast(U16)[:, KP:R])
-        quantize_x(1, 64)
         nc.vector.tensor_copy(staged[:, 0:J].bitcast(I32), picked_s[:].bitcast(I32))
+        for a in range(2):
+            deal(w4_ds[a][:], w4_s[:, a, KP:R])
+        deal(w4_dw[0][:], w4_w[0][:].bitcast(U16)[:, KP:R])
+        grouped = [sb.tile([P, P, PACK], BF16, name=f"x_g1{h}", align_bytes=64) for h in range(2)]
+        round_and_interleave(nc.scalar.copy, grouped[0][:], x_raw[1][:, :, 0:P])
+        round_and_interleave(nc.vector.tensor_copy, grouped[1][:, 0:112], x_raw[1][:, :, P : P + 112])
+        round_and_interleave(nc.scalar.copy, grouped[1][:, 112:P], x_raw[1][:, :, P + 112 : 2 * P])
+        x_q[1, 0] = quantize("x10", grouped[0][:].rearrange("p m t -> p (m t)"), P)
+        x_q[1, 1] = quantize("x11", grouped[1][:].rearrange("p m t -> p (m t)"), P)
         nc.vector.tensor_copy(staged[:, J:].bitcast(I32), planes[:, 2 * J :].bitcast(I32))
+        deal(w4_dw[1][:], w4_w[1][:].bitcast(U16)[:, KP:R])
 
         def move(a, r):
             if a == 0:
@@ -130,8 +137,6 @@ def tile_list_mlat_qf_mask_kernel(
             mask.append(sb.tile([P, J], F32, name=f"mask{h}", align_bytes=64))
             nc.sync.dma_start(out=mask[h][:], in_=msk[h * P : (h + 1) * P, :])
 
-        deal(w4_ds[1][:], w4_s[:, 1, KP:R])
-        deal(w4_dw[1][:], w4_w[1][:].bitcast(U16)[:, KP:R])
 
         picked_pairs = ov.tile([P, J], U32, name="picked_pairs", align_bytes=64, offset=1280)
         for c in range(2):

@@ -48,8 +48,8 @@ def tile_list_mlat_qf_mask_kernel(
         offsets = sb.tile([P, J // 16], U16, name="offsets")
         tab_s = sb.tile([P, T], U8, name="tab_s", align_bytes=64)
         w4_s = sb.tile([P, 2, R], U8, name="w4_s", align_bytes=64)
-        planes = sb.tile([P, 2 * J + N], U8, name="planes", align_bytes=64)
-        staged = ov.tile([P, J + N], U8, name="staged", align_bytes=64, offset=5120)
+        planes = sb.tile([P, 2, J + P], U8, name="planes", align_bytes=64)
+        staged = sb.tile([P, J + P], U8, name="staged", align_bytes=64)
         x_raw = [ov.tile([P, PACK, M], F32, name="x_raw0", align_bytes=64, offset=5120), ov.tile([P, PACK, M], F32, name="x_raw1", align_bytes=64, offset=0)]
         w4_w = [sb.tile([P, 2 * R], U8, name=f"w4_w{a}", align_bytes=64) for a in range(2)]
         tab_w = sb.tile([P, T], I32, name="tab_w", align_bytes=64)
@@ -70,12 +70,12 @@ def tile_list_mlat_qf_mask_kernel(
             nc.sync.dma_start(out=w4_w[a][:].bitcast(I32), in_=w4_words[a].bitcast(I32))
 
         nc.sync.dma_start(offsets[:], offs)
-        nc.scalar.dma_start(out=tab_s[96:P, :].bitcast(I32), in_=tab_scales.bitcast(I32).rearrange("a q n -> (a q) n"))
+        nc.scalar.dma_start(out=tab_s[96:P, :].bitcast(I32), in_=tab_scales.bitcast(I32).rearrange("a q n -> q a n"))
         load_x(0)
         load_scale_rows(nc.sync, w4_s, w4_scales)
         load_w4(0)
         load_x(1)
-        nc.sync.dma_start(out=planes[112:P, 2 * J :].bitcast(I32), in_=wv4_scales.bitcast(I32)[0])
+        nc.sync.dma_start(out=staged[96:P, J:].bitcast(I32), in_=wv4_scales.bitcast(I32)[0].rearrange("q (g n) -> (q g) n", g=2))
         load_w4(1)
         nc.sync.dma_start(out=tab_w[:], in_=tab_words[0].rearrange("p t b -> p (t b)").bitcast(I32))
         picked_s = sb.tile([P, J], U8, name="picked_s", align_bytes=64)
@@ -90,12 +90,11 @@ def tile_list_mlat_qf_mask_kernel(
 
         x_q = {}
 
-        def quantize_x(a, split):
+        def quantize_x(a):
             grouped = [sb.tile([P, P, PACK], BF16, name=f"x_g{a}{h}", align_bytes=64) for h in range(2)]
-            round_and_interleave(nc.vector.tensor_copy, grouped[0][:], x_raw[a][:, :, 0:P])
-            if split:
-                round_and_interleave(nc.vector.tensor_copy, grouped[1][:, 0:split], x_raw[a][:, :, P : P + split])
-            round_and_interleave(nc.scalar.copy, grouped[1][:, split:P], x_raw[a][:, :, P + split : 2 * P])
+            round_and_interleave(nc.scalar.copy, grouped[0][:], x_raw[a][:, :, 0:P])
+            round_and_interleave(nc.vector.tensor_copy, grouped[1][:, 0:112], x_raw[a][:, :, P : P + 112])
+            round_and_interleave(nc.scalar.copy, grouped[1][:, 112:P], x_raw[a][:, :, P + 112 : 2 * P])
             for h in range(2):
                 x_q[a, h] = quantize(f"x{a}{h}", grouped[h][:].rearrange("p m t -> p (m t)"), P)
 
@@ -104,38 +103,26 @@ def tile_list_mlat_qf_mask_kernel(
 
         w4_dw = [sb.tile([P, KP], U16, name=f"w4_dw{a}", align_bytes=64) for a in range(2)]
         w4_ds = [sb.tile([P, KP], U8, name="w4_ds0", align_bytes=64), sb.tile([P, KP], U8, name="w4_ds1", align_bytes=64)]
-        quantize_x(0, 0)
         nc.vector.tensor_copy(staged[:, 0:J].bitcast(I32), picked_s[:].bitcast(I32))
+        quantize_x(0)
         for a in range(2):
             deal(w4_ds[a][:], w4_s[:, a, KP:R])
         deal(w4_dw[0][:], w4_w[0][:].bitcast(U16)[:, KP:R])
-        grouped = [sb.tile([P, P, PACK], BF16, name=f"x_g1{h}", align_bytes=64) for h in range(2)]
-        round_and_interleave(nc.scalar.copy, grouped[0][:], x_raw[1][:, :, 0:P])
-        round_and_interleave(nc.vector.tensor_copy, grouped[1][:, 0:112], x_raw[1][:, :, P : P + 112])
-        round_and_interleave(nc.scalar.copy, grouped[1][:, 112:P], x_raw[1][:, :, P + 112 : 2 * P])
-        x_q[1, 0] = quantize("x10", grouped[0][:].rearrange("p m t -> p (m t)"), P)
-        x_q[1, 1] = quantize("x11", grouped[1][:].rearrange("p m t -> p (m t)"), P)
-        nc.vector.tensor_copy(staged[:, J:].bitcast(I32), planes[:, 2 * J :].bitcast(I32))
+        quantize_x(1)
         deal(w4_dw[1][:], w4_w[1][:].bitcast(U16)[:, KP:R])
 
-        def move(a, r):
-            if a == 0:
-                nc.sync.dma_start(out=planes[r:P:32, 0:J].bitcast(I32), in_=picked_s[96 + r : 112 : 4, :].bitcast(I32))
-            else:
-                nc.sync.dma_start(out=planes[r:P:32, J:].bitcast(I32), in_=staged[112 + r : P : 4, :].bitcast(I32))
-
-        for r in range(2):
-            move(0, r)
         nc.sync.dma_start(out=wv8_raw[:], in_=wv8.rearrange("(p t) n -> p t n", t=PACK))
-        nc.sync.dma_start(out=wv4_w[:].bitcast(I32), in_=wv4_words[0].bitcast(I32))
-        for r in range(4):
-            move(1, r)
-        for r in range(2, 4):
-            move(0, r)
+        for g in range(2):
+            cols = slice(g * P // 2, (g + 1) * P // 2)
+            nc.sync.dma_start(out=wv4_w[:].bitcast(I32)[:, cols], in_=wv4_words[0].bitcast(I32)[:, cols])
+        for q in (0, 2, 1, 3):
+            nc.sync.dma_start(out=planes[32 * q : 32 * q + 4].bitcast(I32), in_=staged[96 + 8 * q : 104 + 8 * q, :].bitcast(I32))
         mask = []
         for h in range(2):
             mask.append(sb.tile([P, J], F32, name=f"mask{h}", align_bytes=64))
-            nc.sync.dma_start(out=mask[h][:], in_=msk[h * P : (h + 1) * P, :])
+            for c in range(2):
+                cols = slice(c * J // 2, (c + 1) * J // 2)
+                nc.sync.dma_start(out=mask[h][:, cols], in_=msk[h * P : (h + 1) * P, cols])
 
 
         picked_pairs = ov.tile([P, J], U32, name="picked_pairs", align_bytes=64, offset=1280)
@@ -154,8 +141,8 @@ def tile_list_mlat_qf_mask_kernel(
             round_and_interleave(nc.vector.tensor_copy, wv8_g[:, g], wv8_raw[:, :, g * P : (g + 1) * P])
 
         direct = [ps.tile([P, KP], F32, name=f"direct{h}", tag=f"bank{h}") for h in range(2)]
-        dealt = [ps.tile([P, PACK, P], F32, name=f"dealt{h}", tag=("bank2", "bank0")[h]) for h in range(2)]
-        turned = [ps.tile([P, 2, P], F32, name=f"turned{h}") for h in range(2)]
+        dealt = [ps.tile([P, PACK, P], F32, name=f"dealt{h}", tag=("bank2", "bank4")[h]) for h in range(2)]
+        turned = [ps.tile([P, 2, P], F32, name=f"turned{h}", tag=f"bank{5 + h}") for h in range(2)]
         qa_g = [sb.tile([P, 2, P, PACK], BF16, name=f"qa_g{h}", align_bytes=64) for h in range(2)]
 
         def project_direct(a, h):
@@ -179,19 +166,19 @@ def tile_list_mlat_qf_mask_kernel(
                     lhsT_scale=w4_ds[a][:, P * t : P * (t + 1)],
                     rhs=codes[:].bitcast(FP8X4),
                     rhs_scale=scales[:],
-                    start=(a == 0 and t == 0),
-                    stop=(a == 1 and t == PACK - 1),
+                    start=(a == h and t == 0),
+                    stop=(a != h and t == PACK - 1),
                 )
 
         for a in range(2):
             for h in range(2):
                 project_direct(a, h)
             project_dealt(a, 0)
+        for a in (1, 0):
+            project_dealt(a, 1)
         rounded = [sb.tile([P, 2, P, 2], BF16, name=f"qa_r{h}", align_bytes=64) for h in range(2)]
         for h in range(2):
             nc.scalar.copy(out=rounded[h][:], in_=direct[h][:].rearrange("m (p u e) -> m u p e", u=2, e=2))
-        for a in range(2):
-            project_dealt(a, 1)
         for h in range(2):
             pairs = rounded[h][:].rearrange("m u p e -> m (u p e)").bitcast(F32)
             for u in range(2):
@@ -200,52 +187,84 @@ def tile_list_mlat_qf_mask_kernel(
             nc.scalar.copy(out=qa_g[h][:, 1], in_=dealt[h][:].rearrange("p t m -> p m t"))
             nc.scalar.copy(out=qa_g[h][:, 0].bitcast(F32), in_=turned[h][:].rearrange("p u m -> p m u"))
 
-        vv = [ps.tile([P, J], F32, name=f"vv{g}", tag=("bank3", "bank1")[g]) for g in range(2)]
+        H = J // 2
+        vv = [
+            [ps.tile([P, H], F32, name=f"vv0{c}", tag=("bank3", "bank0")[c])[:] for c in range(2)],
+            [ps.tile([P, J], F32, name="vv1", tag="bank1")[:]],
+        ]
         for g in range(2):
-            nc.tensor.matmul_mx(
-                out=vv[g][:],
-                lhsT=wv4_w[:, 2 * P * g : 2 * P * (g + 1)].bitcast(FP4X4),
-                lhsT_scale=planes[:, 2 * J + P * g : 2 * J + P * (g + 1)],
-                rhs=picked_w[:, 1, :].bitcast(FP4X4),
-                rhs_scale=planes[:, J : 2 * J],
-                start=True,
-                stop=False,
-            )
-        sc = [ps.tile([P, J], F32, name=f"sc{h}") for h in range(2)]
-        for g in range(2):
-            codes, scales = quantize(f"wv8{g}", wv8_g[:, g].rearrange("p n t -> p (n t)"), P)
-            nc.tensor.matmul_mx(
-                out=vv[g][:],
-                lhsT=codes[:].bitcast(FP8X4),
-                lhsT_scale=scales[:],
-                rhs=picked_w[:, 0, :].bitcast(FP4X4),
-                rhs_scale=planes[:, 0:J],
-                start=False,
-                stop=True,
-            )
-            for c in range(2):
-                cols = slice(c * J // 2, (c + 1) * J // 2)
-                values = sb.tile([P, J // 2], F32, name=f"values{g}{c}")
-                nc.scalar.copy(out=values[:], in_=vv[g][:, cols])
-                nc.sync.dma_start(out=out_1[g * P : (g + 1) * P, cols], in_=values[:])
-        for h in range(2):
-            codes = ov.tile([P, 2 * P], U32, name=f"qa{h}_c", align_bytes=64, offset=10240 + 1024 * h)
-            codes, scales = quantize(f"qa{h}", qa_g[h][:].rearrange("p b m t -> p (b m t)"), 2 * P, codes)
-            for b in (1, 0):
+            width = J // len(vv[g])
+            for c, bank in enumerate(vv[g]):
                 nc.tensor.matmul_mx(
-                    out=sc[h][:],
-                    lhsT=codes[:, b * P : (b + 1) * P].bitcast(FP8X4),
-                    lhsT_scale=scales[:, b * P : (b + 1) * P],
-                    rhs=picked_w[:, b, :].bitcast(FP4X4),
-                    rhs_scale=planes[:, b * J : (b + 1) * J],
-                    start=(b == 1),
-                    stop=(b == 0),
+                    out=bank,
+                    lhsT=wv4_w[:, 2 * P * g : 2 * P * (g + 1)].bitcast(FP4X4),
+                    lhsT_scale=planes[:, g, J:],
+                    rhs=picked_w[:, 1, c * width : (c + 1) * width].bitcast(FP4X4),
+                    rhs_scale=planes[:, 1, c * width : (c + 1) * width],
+                    start=True,
+                    stop=False,
                 )
+        sc = [
+            [ps.tile([P, H], F32, name=f"sc{h}{c}", tag=(("bank2", "bank4"), ("bank7", "bank5"))[h][c]) for c in range(2)]
+            for h in range(2)
+        ]
+
+        def close_values(g):
+            codes, scales = quantize(f"wv8{g}", wv8_g[:, g].rearrange("p n t -> p (n t)"), P)
+            width = J // len(vv[g])
+            step = (P, J)[g]
+            for j in range(0, J, step):
+                nc.tensor.matmul_mx(
+                    out=vv[g][j // width][:, j % width : j % width + step],
+                    lhsT=codes[:].bitcast(FP8X4),
+                    lhsT_scale=scales[:],
+                    rhs=picked_w[:, 0, j : j + step].bitcast(FP4X4),
+                    rhs_scale=planes[:, 0, j : j + step],
+                    start=False,
+                    stop=(j + step) % width == 0,
+                )
+
+        def store_values(g, c):
+            cols = slice(c * J // 2, (c + 1) * J // 2)
+            values = sb.tile([P, J // 2], F32, name=f"values{g}{c}")
+            nc.scalar.copy(out=values[:], in_=vv[0][c] if g == 0 else vv[1][0][:, cols])
+            nc.sync.dma_start(out=out_1[g * P : (g + 1) * P, cols], in_=values[:])
+
+        def quantize_qa(h):
+            codes = ov.tile([P, 2 * P], U32, name=f"qa{h}_c", align_bytes=64, offset=10240 + 1024 * h)
+            return quantize(f"qa{h}", qa_g[h][:].rearrange("p b m t -> p (b m t)"), 2 * P, codes)
+
+        def score_passes(bank, qa, lo, hi, width):
+            codes, scales = qa
+            for b in (1, 0):
+                for j in range(lo, hi, width):
+                    nc.tensor.matmul_mx(
+                        out=bank[:, j - lo : j - lo + width],
+                        lhsT=codes[:, b * P : (b + 1) * P].bitcast(FP8X4),
+                        lhsT_scale=scales[:, b * P : (b + 1) * P],
+                        rhs=picked_w[:, b, j : j + width].bitcast(FP4X4),
+                        rhs_scale=planes[:, b, j : j + width],
+                        start=(b == 1 and j == lo),
+                        stop=(b == 0 and j + width == hi),
+                    )
+
+        def store_scores(h, bank, lo, hi, at):
+            scores = sb.tile([P, hi - lo], F32, name=f"scores{h}_{lo}")
+            nc.vector.scalar_tensor_tensor(
+                out=scores[:], in0=bank[:, at : at + hi - lo], scalar=SCORE_SCALE, in1=mask[h][:, lo:hi], op0=MULT, op1=ADD
+            )
+            nc.sync.dma_start(out=out_0[h * P : (h + 1) * P, lo:hi], in_=scores[:])
+
+        close_values(0)
+        store_values(0, 0)
+        store_values(0, 1)
+        close_values(1)
+        store_values(1, 0)
+        store_values(1, 1)
+        for h in range(2):
+            qa = quantize_qa(h)
+            for c in range(2):
+                score_passes(sc[h][c], qa, c * H, (c + 1) * H, P)
         for h in range(2):
             for c in range(2):
-                cols = slice(c * J // 2, (c + 1) * J // 2)
-                scores = sb.tile([P, J // 2], F32, name=f"scores{h}{c}")
-                nc.vector.scalar_tensor_tensor(
-                    out=scores[:], in0=sc[h][:, cols], scalar=SCORE_SCALE, in1=mask[h][:, cols], op0=MULT, op1=ADD
-                )
-                nc.sync.dma_start(out=out_0[h * P : (h + 1) * P, cols], in_=scores[:])
+                store_scores(h, sc[h][c], c * H, (c + 1) * H, 0)

@@ -212,7 +212,7 @@ def tile_list_mlat_qf_mask_kernel(
         def close_values(g):
             codes, scales = quantize(f"wv8{g}", wv8_g[:, g].rearrange("p n t -> p (n t)"), P)
             width = J // len(vv[g])
-            step = (P, J)[g]
+            step = width
             for j in range(0, J, step):
                 nc.tensor.matmul_mx(
                     out=vv[g][j // width][:, j % width : j % width + step],
@@ -264,7 +264,7 @@ def tile_list_mlat_qf_mask_kernel(
         for h in range(2):
             qa = quantize_qa(h)
             for c in range(2):
-                score_passes(sc[h][c], qa, c * H, (c + 1) * H, P)
+                score_passes(sc[h][c], qa, c * H, (c + 1) * H, H)
         for h in range(2):
             for c in range(2):
                 store_scores(h, sc[h][c], c * H, (c + 1) * H, 0)

@@ -61,6 +61,7 @@ def tile_list_mlat_qf_mask_kernel(
         nc.vector.memset(tab_s[0:96, :].bitcast(I32), 0)
         nc.vector.memset(planes[:].bitcast(I32), 0)
         make_identity(nc, ident[:])
+        nc.gpsimd.dma_start(out=staged[96:P, J:].bitcast(I32), in_=wv4_scales.bitcast(I32)[0].rearrange("q (g n) -> (q g) n", g=2))
 
         def load_x(a):
             rows = x[a * KP : (a + 1) * KP, :].rearrange("(p t) m -> p t m", t=PACK)
@@ -75,7 +76,6 @@ def tile_list_mlat_qf_mask_kernel(
         load_scale_rows(nc.sync, w4_s, w4_scales)
         load_w4(0)
         load_x(1)
-        nc.sync.dma_start(out=staged[96:P, J:].bitcast(I32), in_=wv4_scales.bitcast(I32)[0].rearrange("q (g n) -> (q g) n", g=2))
         load_w4(1)
         nc.sync.dma_start(out=tab_w[:], in_=tab_words[0].rearrange("p t b -> p (t b)").bitcast(I32))
         picked_s = sb.tile([P, J], U8, name="picked_s", align_bytes=64)
@@ -112,17 +112,13 @@ def tile_list_mlat_qf_mask_kernel(
         deal(w4_dw[1][:], w4_w[1][:].bitcast(U16)[:, KP:R])
 
         nc.sync.dma_start(out=wv8_raw[:], in_=wv8.rearrange("(p t) n -> p t n", t=PACK))
-        for g in range(2):
-            cols = slice(g * P // 2, (g + 1) * P // 2)
-            nc.sync.dma_start(out=wv4_w[:].bitcast(I32)[:, cols], in_=wv4_words[0].bitcast(I32)[:, cols])
+        nc.sync.dma_start(out=wv4_w[:].bitcast(I32), in_=wv4_words[0].bitcast(I32))
         for q in (0, 2, 1, 3):
             nc.sync.dma_start(out=planes[32 * q : 32 * q + 4].bitcast(I32), in_=staged[96 + 8 * q : 104 + 8 * q, :].bitcast(I32))
         mask = []
         for h in range(2):
             mask.append(sb.tile([P, J], F32, name=f"mask{h}", align_bytes=64))
-            for c in range(2):
-                cols = slice(c * J // 2, (c + 1) * J // 2)
-                nc.sync.dma_start(out=mask[h][:, cols], in_=msk[h * P : (h + 1) * P, cols])
+            nc.sync.dma_start(out=mask[h][:], in_=msk[h * P : (h + 1) * P, :])
 
 
         picked_pairs = ov.tile([P, J], U32, name="picked_pairs", align_bytes=64, offset=1280)
@@ -227,7 +223,7 @@ def tile_list_mlat_qf_mask_kernel(
         def store_values(g, c):
             cols = slice(c * J // 2, (c + 1) * J // 2)
             values = sb.tile([P, J // 2], F32, name=f"values{g}{c}")
-            nc.scalar.copy(out=values[:], in_=vv[0][c] if g == 0 else vv[1][0][:, cols])
+            nc.scalar.copy(out=values[:], in_=vv[g][c])
             nc.sync.dma_start(out=out_1[g * P : (g + 1) * P, cols], in_=values[:])
 
         def quantize_qa(h):
@@ -248,23 +244,25 @@ def tile_list_mlat_qf_mask_kernel(
                         stop=(b == 0 and j + width == hi),
                     )
 
-        def store_scores(h, bank, lo, hi, at):
-            scores = sb.tile([P, hi - lo], F32, name=f"scores{h}_{lo}")
-            nc.vector.scalar_tensor_tensor(
-                out=scores[:], in0=bank[:, at : at + hi - lo], scalar=SCORE_SCALE, in1=mask[h][:, lo:hi], op0=MULT, op1=ADD
-            )
-            nc.sync.dma_start(out=out_0[h * P : (h + 1) * P, lo:hi], in_=scores[:])
+        def store_scores(h):
+            scores = sb.tile([P, J], F32, name=f"scores{h}")
+            for c in range(2):
+                cols = slice(c * H, (c + 1) * H)
+                nc.vector.scalar_tensor_tensor(
+                    out=scores[:, cols], in0=sc[h][c][:], scalar=SCORE_SCALE, in1=mask[h][:, cols], op0=MULT, op1=ADD
+                )
+            nc.sync.dma_start(out=out_0[h * P : (h + 1) * P, :], in_=scores[:])
 
         close_values(0)
         store_values(0, 0)
         store_values(0, 1)
         close_values(1)
-        store_values(1, 0)
-        store_values(1, 1)
+        values = sb.tile([P, J], F32, name="values1")
+        nc.scalar.copy(out=values[:], in_=vv[1][0])
+        nc.sync.dma_start(out=out_1[P:N, :], in_=values[:])
         for h in range(2):
             qa = quantize_qa(h)
             for c in range(2):
                 score_passes(sc[h][c], qa, c * H, (c + 1) * H, H)
         for h in range(2):
-            for c in range(2):
-                store_scores(h, sc[h][c], c * H, (c + 1) * H, 0)
+            store_scores(h)

@@ -115,10 +115,8 @@ def tile_list_mlat_qf_mask_kernel(
         nc.sync.dma_start(out=wv4_w[:].bitcast(I32), in_=wv4_words[0].bitcast(I32))
         for q in (0, 2, 1, 3):
             nc.sync.dma_start(out=planes[32 * q : 32 * q + 4].bitcast(I32), in_=staged[96 + 8 * q : 104 + 8 * q, :].bitcast(I32))
-        mask = []
-        for h in range(2):
-            mask.append(sb.tile([P, J], F32, name=f"mask{h}", align_bytes=64))
-            nc.sync.dma_start(out=mask[h][:], in_=msk[h * P : (h + 1) * P, :])
+        mask = sb.tile([P, 2, J], F32, name="mask", align_bytes=64)
+        nc.sync.dma_start(out=mask[:], in_=msk.rearrange("(h p) j -> p h j", h=2))
 
 
         picked_pairs = ov.tile([P, J], U32, name="picked_pairs", align_bytes=64, offset=1280)
@@ -249,9 +247,12 @@ def tile_list_mlat_qf_mask_kernel(
             for c in range(2):
                 cols = slice(c * H, (c + 1) * H)
                 nc.vector.scalar_tensor_tensor(
-                    out=scores[:, cols], in0=sc[h][c][:], scalar=SCORE_SCALE, in1=mask[h][:, cols], op0=MULT, op1=ADD
+                    out=scores[:, cols], in0=sc[h][c][:], scalar=SCORE_SCALE, in1=mask[:, h, cols], op0=MULT, op1=ADD
                 )
-            nc.sync.dma_start(out=out_0[h * P : (h + 1) * P, :], in_=scores[:])
+                if h == 1:
+                    nc.sync.dma_start(out=out_0[P:M, cols], in_=scores[:, cols])
+            if h == 0:
+                nc.sync.dma_start(out=out_0[0:P, :], in_=scores[:])
 
         close_values(0)
         store_values(0, 0)

from contextlib import ExitStack

import concourse.mybir as mybir
from concourse.masks import make_identity

K, R, M, T, N, J = 1024, 1024, 256, 1024, 256, 512
FLOPS = 2 * K * R * M + 2 * R * M * J + 2 * R * N * J

F32 = mybir.dt.float32
BF16 = mybir.dt.bfloat16
I32 = mybir.dt.int32
U32 = mybir.dt.uint32
U16 = mybir.dt.uint16
U8 = mybir.dt.uint8
FP8X4 = mybir.dt.float8_e4m3fn_x4
FP4X4 = mybir.dt.float4_e2m1fn_x4
MULT = mybir.AluOpType.mult
ADD = mybir.AluOpType.add

P = 128
PACK = 4
KP = P * PACK
SCORE_SCALE = 0.03125


def load_scale_rows(queue, planes, scales):
    rows = scales.bitcast(I32).rearrange("a (q r) n -> r q a n", r=4)
    for r in range(4):
        queue.dma_start(out=planes[r:P:32, :, :].bitcast(I32), in_=rows[r])


def round_and_interleave(copy, grouped, raw):
    copy(
        out=grouped.rearrange("p (c i) t -> p c t i", i=4),
        in_=raw.rearrange("p t (c i) -> p c t i", i=4),
    )


def tile_list_mlat_qf_mask_kernel(
    tc, x, w4_words, w4_scales, tab_words, tab_scales, wv8, wv4_words, wv4_scales, msk, offs, out_0, out_1
):
    nc = tc.nc
    with ExitStack() as ctx:
        sb = ctx.enter_context(tc.tile_pool(name="sb", bufs=1))
        ov = ctx.enter_context(tc.tile_pool(name="ov", bufs=1))
        ps = ctx.enter_context(tc.psum_pool(name="ps", bufs=1))

        offsets = sb.tile([P, J // 16], U16, name="offsets")
        tab_s = sb.tile([P, T], U8, name="tab_s", align_bytes=64)
        w4_s = sb.tile([P, 2, R], U8, name="w4_s", align_bytes=64)
        planes = sb.tile([P, 2, J + P], U8, name="planes", align_bytes=64)
        staged = sb.tile([P, J + P], U8, name="staged", align_bytes=64)
        x_raw = [ov.tile([P, PACK, M], F32, name="x_raw0", align_bytes=64, offset=5120), ov.tile([P, PACK, M], F32, name="x_raw1", align_bytes=64, offset=0)]
        w4_w = [sb.tile([P, 2 * R], U8, name=f"w4_w{a}", align_bytes=64) for a in range(2)]
        tab_w = sb.tile([P, T], I32, name="tab_w", align_bytes=64)
        wv8_raw = ov.tile([P, PACK, N], F32, name="wv8_raw", align_bytes=64, offset=10240)
        wv4_w = sb.tile([P, 2 * N], U8, name="wv4_w", align_bytes=64)
        ident = sb.tile([P, P], F32, name="ident")

        nc.vector.memset(w4_s[:].bitcast(I32), 0)
        nc.vector.memset(tab_s[0:96, :].bitcast(I32), 0)
        nc.vector.memset(planes[:].bitcast(I32), 0)
        make_identity(nc, ident[:])
        nc.gpsimd.dma_start(out=staged[96:P, J:].bitcast(I32), in_=wv4_scales.bitcast(I32)[0].rearrange("q (g n) -> (q g) n", g=2))

        def load_x(a):
            rows = x[a * KP : (a + 1) * KP, :].rearrange("(p t) m -> p t m", t=PACK)
            nc.sync.dma_start(out=x_raw[a][:], in_=rows)

        def load_w4(a):
            nc.sync.dma_start(out=w4_w[a][:].bitcast(I32), in_=w4_words[a].bitcast(I32))

        nc.sync.dma_start(offsets[:], offs)
        nc.scalar.dma_start(out=tab_s[96:P, :].bitcast(I32), in_=tab_scales.bitcast(I32).rearrange("a q n -> q a n"))
        load_x(0)
        load_scale_rows(nc.sync, w4_s, w4_scales)
        load_w4(0)
        load_x(1)
        load_w4(1)
        nc.sync.dma_start(out=tab_w[:], in_=tab_words[0].rearrange("p t b -> p (t b)").bitcast(I32))
        picked_s = sb.tile([P, J], U8, name="picked_s", align_bytes=64)
        nc.vector.tensor_copy(picked_s[:], tab_s[:].indirect(offsets[:]))

        def quantize(name, grouped, width, codes=None):
            if codes is None:
                codes = sb.tile([P, width], U32, name=name + "_c", align_bytes=64)
            scales = sb.tile([P, width], U8, name=name + "_s", align_bytes=64)
            nc.vector.quantize_mx(out=codes[:].bitcast(FP8X4), scales=scales[:], in_=grouped)
            return codes, scales

        x_q = {}

        def quantize_x(a):
            grouped = [sb.tile([P, P, PACK], BF16, name=f"x_g{a}{h}", align_bytes=64) for h in range(2)]
            round_and_interleave(nc.scalar.copy, grouped[0][:], x_raw[a][:, :, 0:P])
            round_and_interleave(nc.vector.tensor_copy, grouped[1][:, 0:112], x_raw[a][:, :, P : P + 112])
            round_and_interleave(nc.scalar.copy, grouped[1][:, 112:P], x_raw[a][:, :, P + 112 : 2 * P])
            for h in range(2):
                x_q[a, h] = quantize(f"x{a}{h}", grouped[h][:].rearrange("p m t -> p (m t)"), P)

        def deal(out, in_):
            nc.vector.tensor_copy(out=out.rearrange("p (t m) -> p t m", t=PACK), in_=in_.rearrange("p (m t) -> p t m", t=PACK))

        w4_dw = [sb.tile([P, KP], U16, name=f"w4_dw{a}", align_bytes=64) for a in range(2)]
        w4_ds = [sb.tile([P, KP], U8, name="w4_ds0", align_bytes=64), sb.tile([P, KP], U8, name="w4_ds1", align_bytes=64)]
        nc.vector.tensor_copy(staged[:, 0:J].bitcast(I32), picked_s[:].bitcast(I32))
        quantize_x(0)
        for a in range(2):
            deal(w4_ds[a][:], w4_s[:, a, KP:R])
        deal(w4_dw[0][:], w4_w[0][:].bitcast(U16)[:, KP:R])
        quantize_x(1)
        deal(w4_dw[1][:], w4_w[1][:].bitcast(U16)[:, KP:R])

        nc.sync.dma_start(out=wv8_raw[:], in_=wv8.rearrange("(p t) n -> p t n", t=PACK))
        nc.sync.dma_start(out=wv4_w[:].bitcast(I32), in_=wv4_words[0].bitcast(I32))
        for q in (0, 2, 1, 3):
            nc.sync.dma_start(out=planes[32 * q : 32 * q + 4].bitcast(I32), in_=staged[96 + 8 * q : 104 + 8 * q, :].bitcast(I32))
        mask = sb.tile([P, 2, J], F32, name="mask", align_bytes=64)
        nc.sync.dma_start(out=mask[:], in_=msk.rearrange("(h p) j -> p h j", h=2))


        picked_pairs = ov.tile([P, J], U32, name="picked_pairs", align_bytes=64, offset=1280)
        for c in range(2):
            nc.vector.tensor_copy(
                picked_pairs[:, c * 256 : (c + 1) * 256], tab_w[:].bitcast(U32).indirect(offsets[:, c * 16 : (c + 1) * 16])
            )
        wv8_g = sb.tile([P, 2, P, PACK], BF16, name="wv8_g", align_bytes=64)
        picked_w = sb.tile([P, 2, J], U16, name="picked_w", align_bytes=64)
        for c in range(2):
            nc.vector.tensor_copy(
                out=picked_w[:, :, c * 256 : (c + 1) * 256],
                in_=picked_pairs[:, c * 256 : (c + 1) * 256].bitcast(U16).rearrange("p (j d) -> p d j", d=2),
            )
        for g in range(2):
            round_and_interleave(nc.vector.tensor_copy, wv8_g[:, g], wv8_raw[:, :, g * P : (g + 1) * P])

        direct = [ps.tile([P, KP], F32, name=f"direct{h}", tag=f"bank{h}") for h in range(2)]
        dealt = [ps.tile([P, PACK, P], F32, name=f"dealt{h}", tag=("bank2", "bank4")[h]) for h in range(2)]
        turned = [ps.tile([P, 2, P], F32, name=f"turned{h}", tag=f"bank{5 + h}") for h in range(2)]
        qa_g = [sb.tile([P, 2, P, PACK], BF16, name=f"qa_g{h}", align_bytes=64) for h in range(2)]

        def project_direct(a, h):
            codes, scales = x_q[a, h]
            nc.tensor.matmul_mx(
                out=direct[h][:],
                lhsT=codes[:].bitcast(FP8X4),
                lhsT_scale=scales[:],
                rhs=w4_w[a][:, 0 : 2 * KP].bitcast(FP4X4),
                rhs_scale=w4_s[:, a, 0:KP],
                start=(a == 0),
                stop=(a == 1),
            )

        def project_dealt(a, h):
            codes, scales = x_q[a, h]
            for t in range(PACK):
                nc.tensor.matmul_mx(
                    out=dealt[h][:, t, :],
                    lhsT=w4_dw[a][:, P * t : P * (t + 1)].bitcast(FP4X4),
                    lhsT_scale=w4_ds[a][:, P * t : P * (t + 1)],
                    rhs=codes[:].bitcast(FP8X4),
                    rhs_scale=scales[:],
                    start=(a == h and t == 0),
                    stop=(a != h and t == PACK - 1),
                )

        for a in range(2):
            for h in range(2):
                project_direct(a, h)
            project_dealt(a, 0)
        for a in (1, 0):
            project_dealt(a, 1)
        rounded = [sb.tile([P, 2, P, 2], BF16, name=f"qa_r{h}", align_bytes=64) for h in range(2)]
        for h in range(2):
            nc.scalar.copy(out=rounded[h][:], in_=direct[h][:].rearrange("m (p u e) -> m u p e", u=2, e=2))
        for h in range(2):
            pairs = rounded[h][:].rearrange("m u p e -> m (u p e)").bitcast(F32)
            for u in range(2):
                nc.tensor.transpose(turned[h][:, u, :], pairs[:, u * P : (u + 1) * P], ident[:])
        for h in range(2):
            nc.scalar.copy(out=qa_g[h][:, 1], in_=dealt[h][:].rearrange("p t m -> p m t"))
            nc.scalar.copy(out=qa_g[h][:, 0].bitcast(F32), in_=turned[h][:].rearrange("p u m -> p m u"))

        H = J // 2
        vv = [
            [ps.tile([P, H], F32, name=f"vv0{c}", tag=("bank3", "bank0")[c])[:] for c in range(2)],
            [ps.tile([P, J], F32, name="vv1", tag="bank1")[:]],
        ]
        for g in range(2):
            width = J // len(vv[g])
            for c, bank in enumerate(vv[g]):
                nc.tensor.matmul_mx(
                    out=bank,
                    lhsT=wv4_w[:, 2 * P * g : 2 * P * (g + 1)].bitcast(FP4X4),
                    lhsT_scale=planes[:, g, J:],
                    rhs=picked_w[:, 1, c * width : (c + 1) * width].bitcast(FP4X4),
                    rhs_scale=planes[:, 1, c * width : (c + 1) * width],
                    start=True,
                    stop=False,
                )
        sc = [
            [ps.tile([P, H], F32, name=f"sc{h}{c}", tag=(("bank2", "bank4"), ("bank7", "bank5"))[h][c]) for c in range(2)]
            for h in range(2)
        ]

        def close_values(g):
            codes, scales = quantize(f"wv8{g}", wv8_g[:, g].rearrange("p n t -> p (n t)"), P)
            width = J // len(vv[g])
            step = width
            for j in range(0, J, step):
                nc.tensor.matmul_mx(
                    out=vv[g][j // width][:, j % width : j % width + step],
                    lhsT=codes[:].bitcast(FP8X4),
                    lhsT_scale=scales[:],
                    rhs=picked_w[:, 0, j : j + step].bitcast(FP4X4),
                    rhs_scale=planes[:, 0, j : j + step],
                    start=False,
                    stop=(j + step) % width == 0,
                )

        def store_values(g, c):
            cols = slice(c * J // 2, (c + 1) * J // 2)
            values = sb.tile([P, J // 2], F32, name=f"values{g}{c}")
            nc.scalar.copy(out=values[:], in_=vv[g][c])
            nc.sync.dma_start(out=out_1[g * P : (g + 1) * P, cols], in_=values[:])

        def quantize_qa(h):
            codes = ov.tile([P, 2 * P], U32, name=f"qa{h}_c", align_bytes=64, offset=10240 + 1024 * h)
            return quantize(f"qa{h}", qa_g[h][:].rearrange("p b m t -> p (b m t)"), 2 * P, codes)

        def score_passes(bank, qa, lo, hi, width):
            codes, scales = qa
            for b in (1, 0):
                for j in range(lo, hi, width):
                    nc.tensor.matmul_mx(
                        out=bank[:, j - lo : j - lo + width],
                        lhsT=codes[:, b * P : (b + 1) * P].bitcast(FP8X4),
                        lhsT_scale=scales[:, b * P : (b + 1) * P],
                        rhs=picked_w[:, b, j : j + width].bitcast(FP4X4),
                        rhs_scale=planes[:, b, j : j + width],
                        start=(b == 1 and j == lo),
                        stop=(b == 0 and j + width == hi),
                    )

        def store_scores(h):
            scores = sb.tile([P, J], F32, name=f"scores{h}")
            for c in range(2):
                cols = slice(c * H, (c + 1) * H)
                nc.vector.scalar_tensor_tensor(
                    out=scores[:, cols], in0=sc[h][c][:], scalar=SCORE_SCALE, in1=mask[:, h, cols], op0=MULT, op1=ADD
                )
                if h == 1:
                    nc.sync.dma_start(out=out_0[P:M, cols], in_=scores[:, cols])
            if h == 0:
                nc.sync.dma_start(out=out_0[0:P, :], in_=scores[:])

        close_values(0)
        store_values(0, 0)
        store_values(0, 1)
        close_values(1)
        values = sb.tile([P, J], F32, name="values1")
        nc.scalar.copy(out=values[:], in_=vv[1][0])
        nc.sync.dma_start(out=out_1[P:N, :], in_=values[:])
        for h in range(2):
            qa = quantize_qa(h)
            for c in range(2):
                score_passes(sc[h][c], qa, c * H, (c + 1) * H, H)
        for h in range(2):
            store_scores(h)
